import numpy as np, ml_dtypes
CORES = [4,20,36,52,68,84,100,116,132,148,164,180,196,212,228,244]
N = 16
RM, R, T = 131072, 8192, 512
CAPP = 64
def entries(a): return a.T.reshape(-1)
def pack(v, P): return np.ascontiguousarray(np.asarray(v, np.int32).reshape(-1, P).T)
def owners(rng, how):
    if how == "alike": return np.stack([rng.permutation(np.repeat(rng.permutation(N)[:T // CAPP], CAPP)) for r in range(N)])
    if how == "full": p = np.repeat(rng.permutation(N)[:T // CAPP], CAPP); return np.stack([rng.permutation(p) for r in range(N)])
    return np.stack([rng.permutation(np.repeat(np.arange(N), CAPP))[:T] for r in range(N)])
def lists(rng, how):
    M = rng.integers(0, N * R, N * RM)
    O1 = owners(rng, how); O2 = rng.permutation(N)[O1] if how in ("alike", "full") else owners(rng, "uniform")
    sl = np.stack([1 + rng.permutation(RM - 2)[:N * T] for o in range(N)])
    if how == "edge": sl[:, 0] = 0; sl[:, 1] = RM - 1
    I = np.zeros((N, T), np.int64); took = np.zeros(N, np.int64)
    for r in range(N):
        for o in range(N): m = np.nonzero(O1[r] == o)[0]; I[r, m] = RM * o + sl[o, took[o]:took[o] + len(m)]; took[o] += len(m)
    A = R * O2 + (np.where(rng.random((N, T)) < 0.5, 0, R - 1) if how == "edge" else rng.integers(0, R, (N, T)))
    if how == "alike": I = RM * O1 + sl[O1, 0]; A = R * O2 + rng.integers(0, R, N)[O1]
    M[I.reshape(-1)] = A.reshape(-1)
    if how == "sorted": I = np.sort(I, axis=1)
    if how == "full":
        I[1::3] = np.sort(I[1::3], axis=1); I[2::3] = np.sort(I[2::3], axis=1).reshape(-1, 16, T // 16).transpose(0, 2, 1).reshape(-1, T)
    return {"mp": np.stack([pack(m, 16) for m in M.reshape(N, RM)]), "idx": np.stack([pack(i, 16) for i in I])}
def setup_inputs(rng):
    return dict({"tab": rng.standard_normal((N, 128, R), dtype=np.float32).astype(ml_dtypes.bfloat16)}, **lists(rng, "uniform"))
def setup_inputs_alike(rng):
    d = setup_inputs(rng); d.update(lists(rng, "alike"))
    for k in ("tab",): d[k] = (d[k].astype(np.float32) * 1048576.0).astype(d[k].dtype)
    return d
def setup_inputs_edge(rng):
    d = setup_inputs(rng); d.update(lists(rng, "edge"))
    for k in ("tab",): d[k] = (d[k].astype(np.float32) * (1 / 1024.0)).astype(d[k].dtype)
    return d
def setup_inputs_full(rng):
    d = setup_inputs(rng); d.update(lists(rng, "full"))
    return d
def setup_inputs_sorted(rng):
    d = setup_inputs(rng); d.update(lists(rng, "sorted"))
    return d
def check_inputs(x):
    bad = []
    if x["mp"].min() < 0 or x["mp"].max() >= N * R: bad.append("mp out of range")
    if x["idx"].min() < 0 or x["idx"].max() >= N * RM: bad.append("idx out of range")
    M = np.concatenate([entries(m) for m in x["mp"]])
    if max(int(np.bincount(entries(a) // RM, minlength=N).max()) for a in x["idx"]) > CAPP: bad.append("more than CAPP entries of a list point into one rank's part of the map")
    if max(int(np.bincount(M[entries(a)] // R, minlength=N).max()) for a in x["idx"]) > CAPP: bad.append("more than CAPP entries of a list have map values in one rank's part of the table")
    return bad
def reference(tab, mp, idx):
    A = np.concatenate(list(tab), axis=1)
    M = np.concatenate([entries(m) for m in mp])
    return {"y": np.stack([A[:, M[entries(idx[r])]] for r in range(N)])}

@@ -1,0 +1,442 @@
+from concourse.bass import DstId, RemoteDMATransfer
+from concourse.mybir import AluOpType as A, AxisListType, ActivationFunctionType as AF
+
+N, K = 16, 4
+NCORES = 256
+I32, F32, B16, U16 = "int32", "float32", "bfloat16", "uint16"
+_SB = {
+    "IX": (4, I32), "MP": (1024, I32), "TAB": (8192, B16), "H1L": (16, I32), "MS1": (16, I32), "LV": (64, F32), "VV": (2, F32),
+    "LM": (8, I32), "H3L": (16, I32), "MS3": (16, I32), "RES": (512, B16), "LAND": (1024, B16),
+    "ONB": (128, B16), "TRI": (128, B16), "IO1": (64, B16), "IOK": (128, B16), "IDF": (128, F32), "T8": (1024, B16),
+    "DI": (128, I32), "DA": (128, I32), "SE1": (128, B16), "SE2": (128, B16), "SEF": (128, F32), "PI": (1, I32), "PJ": (2, I32),
+    "MKH": (8, F32), "ONF": (128, F32), "BIG": (128, F32),
+    "W1": (8, I32), "W2": (8, I32), "W3": (8, I32), "F1": (8, F32), "F2": (8, F32), "F3": (8, F32), "OHA": (112, B16),
+    "OHB": (240, B16), "ZA": (128, F32), "ZB": (64, F32), "ZC": (32, F32), "ZD": (16, F32), "RA": (4, F32), "RB": (8, F32),
+    "OV": (16, F32), "OW": (64, B16), "LF": (512, F32), "LB": (512, B16), "EF": (32, F32), "EB": (32, B16), "KA": (16, I32),
+    "KB": (16, I32), "KC": (16, B16), "OF1": (32, U16), "OF3": (16, U16), "GG": (256, F32), "MM": (256, F32), "PP": (512, F32),
+}
+SCRATCH = {n: ("sbuf", [128, w], d) for n, (w, d) in _SB.items()}
+SCRATCH.update({"P%d" % i: ("psum", [128, 512], F32) for i in range(6)})
+SEMAPHORES = (["a_idx", "a_mpq", "a_mpo", "a_tabq", "a_tabo", "a_h1", "a_h2", "a_rel", "a_h3", "a_h4", "loc",
+               "l_idx", "l_mp", "l_y"] + ["l_t%d" % i for i in range(K)] + ["c%d" % i for i in range(90)])
+_CACHE = {}
+
+
+def _teams(T, topo):
+    if "t" not in _CACHE:
+        out = []
+        for c in T.cores:
+            chip = [d for d in range(NCORES) if d != c and topo.host(d) == topo.host(c) and topo.chip(d) == topo.chip(c)]
+            near = [d for d in chip if topo.die(d) == topo.die(c)]
+            far = [d for d in chip if topo.die(d) != topo.die(c)]
+            out.append([near[0], far[0], near[1], far[1]])
+        _CACHE["t"] = out
+    return _CACHE["t"]
+
+
+def _kk(r, m):
+    return (r // K + m) % K
+
+
+def _bits(mask):
+    return [i for i in range(16) if (mask >> i) & 1]
+
+
+def _mask(bits):
+    return sum(1 << b for b in bits)
+
+
+def rank_program(g, core, T, topo):
+    teams = _teams(T, topo)
+    rank = T.rank_of(core)
+    S, V, TE = T.sem, g.vector, g.tensor
+    used, loc = [0], [0]
+
+    def phase():
+        used[0] += 1
+        return {"s": T.sem["c%d" % (used[0] - 1)], "n": 0}
+
+    def on(ph, inst):
+        inst.then_inc(ph["s"], 1)
+        ph["n"] += 1
+
+    def wait(q, *phs):
+        for ph in phs:
+            if ph["n"]:
+                q.wait_ge(ph["s"], ph["n"])
+
+    def dst(c):
+        rid, pid = topo.addr(c, core)
+        return DstId(rid=rid, pnc=pid)
+
+    def each(items, sem):
+        common = topo.mask(core, items[0][0])
+        for d, _o, _i in items:
+            common &= topo.mask(core, d)
+        b = _bits(common)
+        g.remote_dma_fused([RemoteDMATransfer(dst_ids=[dst(d)], dma_engine_mask=_mask(b[2 * n:2 * n + 2]), remote_sem=sem, src=i, dst=o)
+                            for n, (d, o, i) in enumerate(items)], local_sem=S.loc)
+        loc[0] += 2 * len(items)
+
+    def same(dests, buf, sem, bits):
+        g.remote_dma_fused([RemoteDMATransfer(dst_ids=[dst(d) for d in dests], dma_engine_mask=_mask(bits), remote_sem=sem,
+                                              srcs=[buf], dsts=[buf for _d in dests])], local_sem=S.loc)
+        loc[0] += len(bits)
+
+    def ranks(C, J, OH, PS, out, pre):
+        z, w = (C - 1) * J, C * J
+        pm = phase()
+        wait(TE, *pre)
+        for d in range(C):
+            on(pm, TE.matmul(PS[:, 0:w], T.TRI[:] if d == 0 else T.ONB[:], OH[:, z - d * J:z - d * J + w], d == 0, d == C - 1))
+
+        def finish():
+            p = phase()
+            wait(V, pm)
+            on(p, V.tensor_tensor(T.ZA[:, 0:w], PS[:, 0:w], OH[:, z:z + w], A.mult))
+            cur, j, n, tmp = T.ZA, J, w, [T.ZB, T.ZC, T.ZD]
+            while j > 1:
+                wait(V, p)
+                p = phase()
+                o = out if j == 2 else tmp.pop(0)
+                on(p, V.tensor_tensor(o[:, 0:n // 2], cur[:, 0:n:2], cur[:, 1:n:2], A.add))
+                cur, j, n = o, j // 2, n // 2
+            return p
+        return finish
+
+    if rank is not None:
+        team = teams[rank]
+        par = (rank % K) & 1
+        onchip = _bits(topo.mask(core, team[0]))
+        nq, nh = len(onchip) // K, len(onchip) // 2
+        g.sync.dma_start(T.IX[:], T.idx[:]).then_inc(S.l_idx, 16)
+        g.scalar.dma_start(T.MP[:], T.mp[:]).then_inc(S.l_mp, 16)
+        g.sync.wait_ge(S.l_mp, 16)
+        tq = [T.TAB[:, 2048 * i:2048 * i + 2048] for i in range(K)]
+        for i in range(K):
+            g.sync.dma_start(tq[i], T.tab[:, 2048 * i:2048 * i + 2048]).then_inc(T.sem["l_t%d" % i], 16)
+        c0 = phase()
+        on(c0, V.memset(T.ONB[:], 1.0))
+        on(c0, V.memset(T.ONF[:], 1.0))
+        on(c0, V.memset(T.OHA[:, 0:48], 0.0))
+        on(c0, V.memset(T.OHB[:, 0:112], 0.0))
+        g.wait_ge(S.l_idx, 16)
+        same(team, T.IX[:], S.a_idx, onchip[:nh])
+        g.wait_ge(S.l_mp, 16)
+        g.remote_dma_fused([RemoteDMATransfer(dst_ids=[dst(h)], dma_engine_mask=_mask(onchip[nq * i:nq * i + nq]), remote_sem=S.a_mpq,
+                                              src=T.MP[:, 256 * i:256 * i + 256], dst=T.MP[:, 256 * i:256 * i + 256])
+                            for i, h in enumerate(team)], local_sem=S.loc)
+        loc[0] += len(onchip)
+        c1 = phase()
+        wait(g, c0)
+        on(c1, g.affine_select(T.TRI[:], T.ONB[:], [[1, 128]], A.is_ge, 0.0, 0, -1))
+        on(c1, g.affine_select(T.IDF[:], T.ONF[:], [[-1, 128]], A.is_equal, 0.0, 0, 1))
+        on(c1, g.iota(T.IOK[:], [[1, 128]], 0, 0, allow_small_or_imprecise_dtypes=True))
+        on(c1, g.iota(T.PI[:], [[0, 1]], 0, 1))
+        on(c1, g.iota(T.BIG[:], [[0, 8], [1, 16]], 0, 0, allow_small_or_imprecise_dtypes=True))
+        for i, h in enumerate(team):
+            g.wait_ge(T.sem["l_t%d" % i], 16)
+            same([h], tq[i], S.a_tabq, onchip)
+        c2 = phase()
+        wait(V, c0, c1)
+        on(c2, V.tensor_scalar(T.PJ[:, 0:1], T.PI[:], 3, None, A.arith_shift_right))
+        on(c2, V.tensor_scalar(T.PJ[:, 1:2], T.PI[:], 7, None, A.bitwise_and))
+        wait(V, c2)
+        c3 = phase()
+        on(c3, V.tensor_copy(T.VV[:, 0:1], T.PJ[:, 0:1]))
+        for h in range(8):
+            on(c3, V.tensor_scalar(T.MKH[:, h:h + 1], T.PJ[:, 1:2], float(h), None, A.is_equal))
+        wait(V, c3)
+        c4 = phase()
+        on(c4, V.tensor_scalar(T.SEF[:], T.BIG[:], T.VV[:, 0:1], None, A.is_equal))
+        V.wait_ge(S.l_idx, 16)
+        p = phase()
+        on(p, V.tensor_scalar(T.W1[:, 0:4], T.IX[:], 17, None, A.arith_shift_right))
+        wait(V, p)
+        p, p2 = phase(), phase()
+        for j in range(N):
+            on(p, V.tensor_scalar(T.OHA[:, 48 + j:112:16], T.W1[:, 0:4], float(j), None, A.is_equal))
+        on(p2, V.tensor_scalar(T.W2[:, 0:4], T.W1[:, 0:4], 1, None, A.bitwise_and))
+        on(p2, V.tensor_scalar(T.W3[:, 0:4], T.W1[:, 0:4], 1, None, A.arith_shift_right))
+        fin = ranks(4, N, T.OHA, T.P0, T.RA, [c0, c1, p])
+        wait(V, p2)
+        p3, p4 = phase(), phase()
+        on(p4, V.tensor_copy(T.F2[:, 0:4], T.W3[:, 0:4]))
+        s, o = (-64.0, 63.0) if par else (64.0, -1.0)
+        on(p3, V.tensor_scalar(T.F1[:, 0:4], T.W2[:, 0:4], s, o, A.mult, A.add))
+        pr = fin()
+        wait(V, pr, p3)
+        p = phase()
+        on(p, V.tensor_tensor(T.F3[:, 0:4], T.F1[:, 0:4], T.RA[:], A.add))
+        wait(V, p, p4)
+        p, pq = phase(), phase()
+        for c in range(4):
+            on(p, V.tensor_scalar(T.LF[:, 128 * c:128 * c + 128], T.IOK[:], T.F3[:, c:c + 1], None, A.is_equal))
+            on(pq, V.tensor_scalar(T.MM[:, 8 * c:8 * c + 8], T.IOK[:, 0:8], T.F2[:, c:c + 1], None, A.is_equal))
+        wait(TE, p)
+        pt = phase()
+        for c in range(4):
+            on(pt, TE.transpose(T.P1[:, 128 * c:128 * c + 128], T.LF[:, 128 * c:128 * c + 128], T.IDF[:]))
+        wait(V, pt)
+        pt2 = phase()
+        on(pt2, V.tensor_copy(T.PP[:], T.P1[:]))
+        V.wait_ge(S.a_rel, len(onchip))
+        wait(V, pq)
+        p = phase()
+        on(p, V.tensor_scalar(T.W1[:], T.LM[:], 13, None, A.arith_shift_right))
+        wait(V, p)
+        p, p2 = phase(), phase()
+        for j in range(N):
+            on(p, V.tensor_scalar(T.OHB[:, 112 + j:240:16], T.W1[:], float(16 + j), None, A.is_equal))
+        on(p2, V.tensor_scalar(T.F1[:], T.W1[:], 64.0, -1025.0, A.mult, A.add))
+        fin = ranks(8, N, T.OHB, T.P2, T.RB, [p])
+        pr = fin()
+        wait(V, pr, p2)
+        p = phase()
+        on(p, V.tensor_tensor(T.F2[:], T.F1[:], T.RB[:], A.add))
+        wait(TE, p, pt2)
+        pm = phase()
+        for c in range(4):
+            on(pm, TE.matmul(T.P3[:, 8 * c:8 * c + 8], T.PP[:, 128 * c:128 * c + 128], T.F2[:], True, True))
+        wait(V, pm)
+        p = phase()
+        on(p, V.tensor_tensor(T.ZB[:, 0:32], T.P3[:, 0:32], T.MM[:, 0:32], A.mult))
+        for o, i, n in ((T.ZC, T.ZB, 32), (T.ZD, T.ZC, 16), (T.F1, T.ZD, 8)):
+            wait(V, p)
+            p = phase()
+            on(p, V.tensor_tensor(o[:, 0:n // 2], i[:, 0:n:2], i[:, 1:n:2], A.add))
+        wait(V, p)
+        p = phase()
+        for h in range(8):
+            on(p, V.tensor_scalar(T.EF[:, 4 * h:4 * h + 4], T.F1[:, 0:4], T.MKH[:, h:h + 1], None, A.mult))
+        wait(TE, c4, p)
+        pm = phase()
+        on(pm, TE.matmul(T.P4[:, 0:32], T.SEF[:], T.EF[:], True, True))
+        wait(V, pm)
+        po = phase()
+        on(po, V.tensor_copy(T.OF1[:], T.P4[:, 0:32]))
+        p1, p2 = phase(), phase()
+        for q in (V, g.scalar):
+            wait(q, po)
+            q.wait_ge(S.a_h4, 2 * N)
+        on(p1, V.tensor_copy(T.RES[:, 0:256], T.LAND[:].indirect(T.OF1[:, 0:16])))
+        on(p2, g.scalar.activation(T.RES[:, 256:512], T.LAND[:].indirect(T.OF1[:, 16:32]), AF.Copy))
+        wait(g.sync, p1)
+        g.sync.dma_start(T.y[:, 0:256], T.RES[:, 0:256]).then_inc(S.l_y, 16)
+        wait(g.scalar, p2)
+        g.scalar.dma_start(T.y[:, 256:512], T.RES[:, 256:512]).then_inc(S.l_y, 16)
+        g.sync.wait_ge(S.l_y, 32)
+        g.wait_ge(S.loc, loc[0])
+        return
+
+    mine = [r for r in range(N) if core in teams[r]]
+    if not mine:
+        return
+    me = mine[0]
+    team = teams[me]
+    k = team.index(core)
+    others = [h for h in team if h != core]
+    u = me % K
+    par = u & 1
+    served = [r for r in range(N) if _kk(r, me) == k]
+    classes = [K * k + j for j in range(K)]
+    to = [teams[m][_kk(me, m)] for m in classes]
+    onchip = _bits(topo.mask(core, T.cores[me]))
+    off = _bits(topo.mask(core, teams[(me + 1) % N][0]))
+    high = [b for b in onchip if b not in off]
+    nq, nh = len(onchip) // K, len(onchip) // 2
+
+    c0 = phase()
+    on(c0, V.memset(T.ONB[:], 1.0))
+    on(c0, V.memset(T.OHA[:, 0:12], 0.0))
+    on(c0, V.memset(T.OHB[:, 0:28], 0.0))
+    on(c0, V.memset(T.ONF[:], 1.0))
+    on(c0, V.memset(T.BIG[0:1, :], 131072.0))
+    on(c0, V.memset(T.T8[0:16, :], 1.0))
+    c1, c1b, c1c = phase(), phase(), phase()
+    on(c1, g.iota(T.DI[:], [[-1, 128]], 128, 1))
+    on(c1, g.iota(T.PI[:], [[0, 1]], 0, 1))
+    on(c1, g.iota(T.IO1[:], [[1, 64]], 1, 0, allow_small_or_imprecise_dtypes=True))
+    wait(g, c0)
+    on(c1b, g.affine_select(T.TRI[:], T.ONB[:], [[1, 128]], A.is_ge, 0.0, 0, -1))
+    on(c1c, g.affine_select(T.IDF[:], T.ONF[:], [[-1, 128]], A.is_equal, 0.0, 0, 1))
+    on(c1c, g.iota(T.IOK[:], [[1, 128]], 128, 0, allow_small_or_imprecise_dtypes=True))
+    on(c1c, g.affine_select(T.T8[0:16, :], T.T8[0:16, :], [[-16, 8], [1, 128]], A.is_equal, 0.0, 0, -1))
+    wait(V, c0, c1)
+    c2 = phase()
+    on(c2, V.tensor_scalar(T.DA[:], T.DI[:], 15, None, A.bitwise_and))
+    on(c2, V.tensor_scalar(T.PJ[:, 0:1], T.PI[:], 4, None, A.arith_shift_right))
+    wait(V, c2)
+    c3 = phase()
+    on(c3, V.tensor_scalar(T.SEF[:], T.DA[:], 0.0, None, A.is_equal))
+    on(c3, V.tensor_scalar(T.SE1[:], T.DA[:], 0.0, None, A.is_equal))
+    on(c3, V.tensor_scalar(T.SE2[:], T.DA[:], 0.0, 128.0, A.is_equal, A.mult))
+    for h in range(4):
+        on(c3, V.tensor_scalar(T.MKH[:, h:h + 1], T.PJ[:, 0:1], float(h), None, A.is_equal))
+    wait(V, c3)
+    PG = [T.P4, T.P5]
+    wait(TE, c0)
+    cg = phase()
+    for b in range(2):
+        on(cg, TE.matmul(PG[b][:, 0:128], T.ONF[0:1, :], T.BIG[0:1, :], True, False))
+
+    def wrap(PSP, parts, Ebuf, sels, PSW, out, pre, selfs, landing):
+        n = 4 * parts
+        wait(V, pre)
+        pe = phase()
+        for h in range(4):
+            on(pe, V.tensor_scalar(Ebuf[0:64, h:4 * n:4], PSP[0:64, 0:n], T.MKH[0:64, h:h + 1], None, A.mult))
+        wait(TE, c3, pe)
+        pm = phase()
+        for i in range(parts):
+            on(pm, TE.matmul(PSW[:, 0:16], sels[i][0:64, :], Ebuf[0:64, 16 * i:16 * i + 16], i == 0, i == parts - 1))
+        wait(V, pm)
+        po, ps = phase(), phase()
+        on(po, V.tensor_copy(out[:], PSW[:, 0:16]))
+        for j, col in selfs:
+            on(ps, V.tensor_copy(landing[:, col:col + 4], PSW[:, 4 * j:4 * j + 4]))
+        return po, ps
+
+    V.wait_ge(S.a_idx, nh)
+    p = phase()
+    on(p, V.tensor_scalar(T.W1[:, 0:4], T.IX[:], 17, None, A.arith_shift_right))
+    on(p, V.tensor_scalar(T.W2[:, 0:4], T.IX[:], 15, None, A.bitwise_and))
+    on(p, V.tensor_scalar(T.W3[:, 0:4], T.IX[:], 4, 8191, A.arith_shift_right, A.bitwise_and))
+    wait(V, p)
+    p, p2 = phase(), phase()
+    for j in range(K):
+        on(p, V.tensor_scalar(T.OHA[:, 12 + j:28:4], T.W1[:, 0:4], float(classes[j]), None, A.is_equal))
+    on(p2, V.tensor_scalar(T.F1[:, 0:4], T.W2[:, 0:4], 8192.0, 131072.0, A.mult, A.add))
+    fin = ranks(4, K, T.OHA, T.P0, T.RA, [c1b, p])
+    wait(V, p2)
+    p2 = phase()
+    on(p2, V.tensor_tensor(T.F2[:, 0:4], T.F1[:, 0:4], T.W3[:, 0:4], A.add))
+    wait(V, p, p2)
+    p2 = phase()
+    for j in range(K):
+        on(p2, V.tensor_tensor(T.OV[:, j:16:4], T.OHA[:, 12 + j:28:4], T.F2[:, 0:4], A.mult))
+    pr = fin()
+    wait(V, pr)
+    pl = [phase(), phase()]
+    for c in range(4):
+        on(pl[c // 2], V.tensor_scalar(T.LF[:, 64 * c:64 * c + 64], T.IO1[:], T.RA[:, c:c + 1], None, A.is_equal))
+    wait(TE, p2)
+    pm = phase()
+    for c in range(4):
+        if c % 2 == 0:
+            wait(TE, pl[c // 2])
+        on(pm, TE.matmul(T.P1[0:64, 0:4], T.LF[:, 64 * c:64 * c + 64], T.OV[:, 4 * c:4 * c + 4], c == 0, c == 3))
+    land = [4 * (u ^ (m & 1)) for m in classes]
+    po, ps1 = wrap(T.P1, 1, T.EF, [T.SEF], T.P2, T.MS1, pm, [(j, land[j]) for j in range(K) if to[j] == core], T.H1L)
+    g.wait_ge(S.a_mpq, nq)
+    same(others, T.MP[:, 256 * k:256 * k + 256], S.a_mpo, onchip)
+    wait(g, po)
+    each([(to[j], T.H1L[:, land[j]:land[j] + 4], T.MS1[:, 4 * j:4 * j + 4]) for j in range(K) if to[j] != core], S.a_h1)
+
+    n1 = len([r for r in served if teams[r][me // K] != core])
+    V.wait_ge(S.a_h1, 2 * n1)
+    wait(V, ps1)
+    p, pb = phase(), phase()
+    on(p, V.tensor_scalar(T.KA[:], T.H1L[:], 1023, None, A.bitwise_and))
+    on(pb, V.tensor_scalar(T.KB[:], T.H1L[:], 10, None, A.arith_shift_right))
+    wait(V, p)
+    p = phase()
+    on(p, V.tensor_copy(T.OF1[:, 0:16], T.KA[:]))
+    wait(V, pb)
+    pb = phase()
+    on(pb, V.tensor_copy(T.KC[:], T.KB[:]))
+    V.wait_ge(S.a_mpq, nq)
+    V.wait_ge(S.a_mpo, (K - 1) * len(onchip))
+    wait(V, p)
+    pg = [phase(), phase()]
+    for b in range(2):
+        on(pg[b], V.tensor_copy(T.GG[:, 128 * b:128 * b + 128], T.MP[:].indirect(T.OF1[:, 8 * b:8 * b + 8])))
+    wait(TE, c1c, pb)
+    pk = phase()
+    for n in range(8):
+        on(pk, TE.matmul(T.P3[:, 0:2], T.T8[0:16, 128 * n:128 * n + 128], T.KC[0:16, n:16:8], n == 0, n == 7))
+    pgt = [phase(), phase()]
+    wait(TE, cg)
+    for b in range(2):
+        wait(TE, pg[b])
+        on(pgt[b], TE.matmul(PG[b][:, 0:128], T.GG[:, 128 * b:128 * b + 128], T.IDF[:], False, True))
+    wait(V, c1c, pk)
+    pmk = phase()
+    for b in range(2):
+        on(pmk, V.tensor_scalar(T.MM[:, 128 * b:128 * b + 128], T.IOK[:], T.P3[:, b:b + 1], None, A.is_equal))
+    wait(V, pmk)
+    pv = phase()
+    for b in range(2):
+        wait(V, pgt[b])
+        p = phase()
+        on(p, V.tensor_tensor(T.PP[:, 128 * b:128 * b + 128], PG[b][:, 0:128], T.MM[:, 128 * b:128 * b + 128], A.mult))
+        wait(V, p)
+        on(pv, V.tensor_reduce(T.VV[:, b:b + 1], T.PP[:, 128 * b:128 * b + 128], AxisListType.X, A.add))
+    blk = {r: ((r % K) ^ (me & 1)) // 2 for r in served}
+    lv = T.LV[:, 4 * me:4 * me + 1]
+    ps2 = phase()
+    for r in served:
+        if teams[r][0] == core:
+            wait(V, pv)
+            on(ps2, V.tensor_copy(lv, T.VV[:, blk[r]:blk[r] + 1]))
+    wait(g, pv)
+    each([(teams[r][0], lv, T.VV[:, blk[r]:blk[r] + 1]) for r in served if teams[r][0] != core], S.a_h2)
+    g.wait_ge(S.a_tabq, len(onchip))
+    same(others, T.TAB[:, 2048 * k:2048 * k + 2048], S.a_tabo, high)
+
+    if k == 0:
+        n2 = len([m for m in range(N) if teams[m][_kk(me, m)] != core])
+        V.wait_ge(S.a_h2, 2 * n2)
+        wait(V, ps2)
+        p = phase()
+        on(p, V.tensor_copy(T.LM[0:64, :], T.LV[0:64, 4 * par:64:8]))
+        on(p, V.tensor_copy(T.LM[64:128, :], T.LV[64:128, 4 * (1 - par):64:8]))
+        wait(g, p)
+        same(others + [T.cores[me]], T.LM[:], S.a_rel, onchip)
+        wait(V, p)
+    else:
+        V.wait_ge(S.a_rel, len(onchip))
+
+    p = phase()
+    on(p, V.tensor_scalar(T.W1[:], T.LM[:], 13, None, A.arith_shift_right))
+    on(p, V.tensor_scalar(T.W2[:], T.LM[:], 7, 63, A.arith_shift_right, A.bitwise_and))
+    on(p, V.tensor_scalar(T.W3[:], T.LM[:], 127, None, A.bitwise_and))
+    wait(V, p)
+    p = phase()
+    for j in range(K):
+        on(p, V.tensor_scalar(T.OHB[:, 28 + j:60:4], T.W1[:], float(16 + classes[j]), None, A.is_equal))
+    fin = ranks(8, K, T.OHB, T.P0, T.RB, [p])
+    wait(V, p)
+    p2 = phase()
+    for j in range(K):
+        on(p2, V.tensor_tensor(T.OW[:, j:64:8], T.OHB[:, 28 + j:60:4], T.W2[:], A.mult))
+        on(p2, V.tensor_tensor(T.OW[:, 4 + j:64:8], T.OHB[:, 28 + j:60:4], T.W3[:], A.mult))
+    pr = fin()
+    wait(V, pr)
+    pl = [phase() for _ in range(4)]
+    for c in range(8):
+        on(pl[c // 2], V.tensor_scalar(T.LB[:, 64 * c:64 * c + 64], T.IO1[:], T.RB[:, c:c + 1], None, A.is_equal))
+    wait(TE, p2)
+    pm = phase()
+    for c in range(8):
+        if c % 2 == 0:
+            wait(TE, pl[c // 2])
+        on(pm, TE.matmul(T.P1[0:64, 0:8], T.LB[:, 64 * c:64 * c + 64], T.OW[:, 8 * c:8 * c + 8], c == 0, c == 7))
+    po, ps3 = wrap(T.P1, 2, T.EB, [T.SE2, T.SE1], T.P2, T.MS3, pm, [(j, 4 * u) for j in range(K) if to[j] == core], T.H3L)
+    wait(g, po)
+    each([(to[j], T.H3L[:, 4 * u:4 * u + 4], T.MS3[:, 4 * j:4 * j + 4]) for j in range(K) if to[j] != core], S.a_h3)
+
+    V.wait_ge(S.a_h3, 2 * n1)
+    wait(V, ps3)
+    p = phase()
+    on(p, V.tensor_copy(T.OF3[:], T.H3L[:]))
+    pc = [phase(), phase()]
+    for b, q in enumerate([V, g.scalar]):
+        wait(q, p)
+        q.wait_ge(S.a_tabq, len(onchip))
+        q.wait_ge(S.a_tabo, (K - 1) * len(high))
+        o, i = T.RES[:, 128 * b:128 * b + 128], T.TAB[:].indirect(T.OF3[:, 8 * b:8 * b + 8])
+        on(pc[b], V.tensor_copy(o, i) if b == 0 else g.scalar.activation(o, i, AF.Copy))
+    wait(g, pc[0], pc[1])
+    each([(T.cores[r], T.LAND[:, 64 * me:64 * me + 64], T.RES[:, 64 * (r % K):64 * (r % K) + 64]) for r in served], S.a_h4)
+    g.wait_ge(S.loc, loc[0])

@@ -5,20 +5,23 @@ N, K = 16, 4
 NCORES = 256
 I32, F32, B16, U16 = "int32", "float32", "bfloat16", "uint16"
 _SB = {
-    "IX": (4, I32), "MP": (1024, I32), "TAB": (8192, B16), "H1L": (16, I32), "MS1": (16, I32), "LV": (64, F32), "VV": (2, F32),
+    "IX": (4, I32), "MP": (1024, I32), "TAB": (8192, B16), "LV": (64, F32), "VV": (2, F32),
     "LM": (8, I32), "H3L": (16, I32), "MS3": (16, I32), "RES": (512, B16), "LAND": (1024, B16),
-    "ONB": (128, B16), "TRI": (128, B16), "IO1": (64, B16), "IOK": (128, B16), "IDF": (128, F32), "T8": (1024, B16),
-    "DI": (128, I32), "DA": (128, I32), "SE1": (128, B16), "SE2": (128, B16), "SEF": (128, F32), "PI": (1, I32), "PJ": (2, I32),
-    "MKH": (8, F32), "ONF": (128, F32), "BIG": (128, F32),
+    "ONB": (128, B16), "TRI": (128, B16), "IO1": (64, B16), "IOK": (128, B16), "IDF": (128, F32), "SHB": (256, B16),
+    "DA": (128, I32), "SE1": (128, B16), "SE2": (128, B16), "SE3": (128, B16), "SEF": (128, F32),
+    "PI": (1, I32), "PJ": (2, I32), "MKH": (8, F32), "ONF": (128, F32), "BIG": (128, F32),
+    "RAW": (16, I32), "RI": (80, I32), "FA": (16, F32), "PB": (48, B16), "KC": (4, B16),
     "W1": (8, I32), "W2": (8, I32), "W3": (8, I32), "F1": (8, F32), "F2": (8, F32), "F3": (8, F32), "OHA": (112, B16),
     "OHB": (240, B16), "ZA": (128, F32), "ZB": (64, F32), "ZC": (32, F32), "ZD": (16, F32), "RA": (4, F32), "RB": (8, F32),
-    "OV": (16, F32), "OW": (64, B16), "LF": (512, F32), "LB": (512, B16), "EF": (32, F32), "EB": (32, B16), "KA": (16, I32),
-    "KB": (16, I32), "KC": (16, B16), "OF1": (32, U16), "OF3": (16, U16), "GG": (256, F32), "MM": (256, F32), "PP": (512, F32),
+    "OW": (64, B16), "LF": (512, F32), "LB": (1024, B16), "EF": (32, F32), "EB": (32, B16),
+    "OF1": (32, U16), "OF3": (16, U16), "GG": (256, F32), "MM": (256, F32), "PP": (512, F32),
 }
 SCRATCH = {n: ("sbuf", [128, w], d) for n, (w, d) in _SB.items()}
 SCRATCH.update({"P%d" % i: ("psum", [128, 512], F32) for i in range(6)})
-SEMAPHORES = (["a_idx", "a_mpq", "a_mpo", "a_tabq", "a_tabo", "a_h1", "a_h2", "a_rel", "a_h3", "a_h4", "loc",
-               "l_idx", "l_mp", "l_y"] + ["l_t%d" % i for i in range(K)] + ["c%d" % i for i in range(90)])
+SCRATCH["IXD"] = ("dram", [128, 4], I32)
+SCRATCH["IXL"] = ("dram", [K, 128, 4], I32)
+SEMAPHORES = (["a_mpq", "a_mpo", "a_tabq", "a_tabo", "a_h1", "a_h2", "a_rel", "a_h3", "a_h4", "loc",
+               "l_ixd", "l_idx", "l_mp", "l_y", "l_in"] + ["l_t%d" % i for i in range(K)] + ["c%d" % i for i in range(90)])
 _CACHE = {}
 
 
@@ -36,6 +39,10 @@ def _teams(T, topo):
 
 def _kk(r, m):
     return (r // K + m) % K
+
+
+def _ks(r, m):
+    return (m // K + r) % K
 
 
 def _bits(mask):
@@ -69,74 +76,83 @@ def rank_program(g, core, T, topo):
         rid, pid = topo.addr(c, core)
         return DstId(rid=rid, pnc=pid)
 
+    def common(cores):
+        m = topo.mask(core, cores[0])
+        for d in cores:
+            m &= topo.mask(core, d)
+        return _bits(m)
+
     def each(items, sem):
-        common = topo.mask(core, items[0][0])
-        for d, _o, _i in items:
-            common &= topo.mask(core, d)
-        b = _bits(common)
+        b = common([d for d, _o, _i in items])
         g.remote_dma_fused([RemoteDMATransfer(dst_ids=[dst(d)], dma_engine_mask=_mask(b[2 * n:2 * n + 2]), remote_sem=sem, src=i, dst=o)
                             for n, (d, o, i) in enumerate(items)], local_sem=S.loc)
         loc[0] += 2 * len(items)
 
-    def same(dests, buf, sem, bits):
+    def same(dests, out, in_, sem, bits):
         g.remote_dma_fused([RemoteDMATransfer(dst_ids=[dst(d) for d in dests], dma_engine_mask=_mask(bits), remote_sem=sem,
-                                              srcs=[buf], dsts=[buf for _d in dests])], local_sem=S.loc)
+                                              srcs=[in_], dsts=[out for _d in dests])], local_sem=S.loc)
         loc[0] += len(bits)
 
-    def ranks(C, J, OH, PS, out, pre):
+    def count(C, J, OH, PS, pre):
         z, w = (C - 1) * J, C * J
         pm = phase()
         wait(TE, *pre)
         for d in range(C):
             on(pm, TE.matmul(PS[:, 0:w], T.TRI[:] if d == 0 else T.ONB[:], OH[:, z - d * J:z - d * J + w], d == 0, d == C - 1))
+        return pm
 
-        def finish():
+    def own(C, J, OH, PS, pm):
+        z, w = (C - 1) * J, C * J
+        p = phase()
+        wait(V, pm)
+        on(p, V.tensor_tensor(T.ZA[:, 0:w], PS[:, 0:w], OH[:, z:z + w], A.mult))
+        return p
+
+    def ranks(C, J, OH, PS, out, pm):
+        p = own(C, J, OH, PS, pm)
+        cur, j, n, tmp = T.ZA, J, C * J, [T.ZB, T.ZC, T.ZD]
+        while j > 1:
+            wait(V, p)
             p = phase()
-            wait(V, pm)
-            on(p, V.tensor_tensor(T.ZA[:, 0:w], PS[:, 0:w], OH[:, z:z + w], A.mult))
-            cur, j, n, tmp = T.ZA, J, w, [T.ZB, T.ZC, T.ZD]
-            while j > 1:
-                wait(V, p)
-                p = phase()
-                o = out if j == 2 else tmp.pop(0)
-                on(p, V.tensor_tensor(o[:, 0:n // 2], cur[:, 0:n:2], cur[:, 1:n:2], A.add))
-                cur, j, n = o, j // 2, n // 2
-            return p
-        return finish
+            o = out if j == 2 else tmp.pop(0)
+            on(p, V.tensor_tensor(o[:, 0:n // 2], cur[:, 0:n:2], cur[:, 1:n:2], A.add))
+            cur, j, n = o, j // 2, n // 2
+        return p
 
     if rank is not None:
         team = teams[rank]
         par = (rank % K) & 1
         onchip = _bits(topo.mask(core, team[0]))
-        nq, nh = len(onchip) // K, len(onchip) // 2
+        nq = len(onchip) // K
+        g.sync.dma_start(T.IXD[:], T.idx[:]).then_inc(S.l_ixd, 16)
         g.sync.dma_start(T.IX[:], T.idx[:]).then_inc(S.l_idx, 16)
         g.scalar.dma_start(T.MP[:], T.mp[:]).then_inc(S.l_mp, 16)
         g.sync.wait_ge(S.l_mp, 16)
         tq = [T.TAB[:, 2048 * i:2048 * i + 2048] for i in range(K)]
         for i in range(K):
             g.sync.dma_start(tq[i], T.tab[:, 2048 * i:2048 * i + 2048]).then_inc(T.sem["l_t%d" % i], 16)
-        c0 = phase()
+        c0, c1 = phase(), phase()
         on(c0, V.memset(T.ONB[:], 1.0))
         on(c0, V.memset(T.ONF[:], 1.0))
         on(c0, V.memset(T.OHA[:, 0:48], 0.0))
         on(c0, V.memset(T.OHB[:, 0:112], 0.0))
-        g.wait_ge(S.l_idx, 16)
-        same(team, T.IX[:], S.a_idx, onchip[:nh])
+        on(c1, g.iota(T.IOK[:], [[1, 128]], 0, 0, allow_small_or_imprecise_dtypes=True))
+        on(c1, g.iota(T.PI[:], [[0, 1]], 0, 1))
+        on(c1, g.iota(T.BIG[:], [[0, 8], [1, 16]], 0, 0, allow_small_or_imprecise_dtypes=True))
+        g.wait_ge(S.l_ixd, 16)
+        where = [teams[m][_kk(rank, m)] for m in range(N)]
+        same(where, T.IXL[rank % K], T.IXD[:], S.a_h1, common(where))
         g.wait_ge(S.l_mp, 16)
         g.remote_dma_fused([RemoteDMATransfer(dst_ids=[dst(h)], dma_engine_mask=_mask(onchip[nq * i:nq * i + nq]), remote_sem=S.a_mpq,
                                               src=T.MP[:, 256 * i:256 * i + 256], dst=T.MP[:, 256 * i:256 * i + 256])
                             for i, h in enumerate(team)], local_sem=S.loc)
         loc[0] += len(onchip)
-        c1 = phase()
         wait(g, c0)
         on(c1, g.affine_select(T.TRI[:], T.ONB[:], [[1, 128]], A.is_ge, 0.0, 0, -1))
         on(c1, g.affine_select(T.IDF[:], T.ONF[:], [[-1, 128]], A.is_equal, 0.0, 0, 1))
-        on(c1, g.iota(T.IOK[:], [[1, 128]], 0, 0, allow_small_or_imprecise_dtypes=True))
-        on(c1, g.iota(T.PI[:], [[0, 1]], 0, 1))
-        on(c1, g.iota(T.BIG[:], [[0, 8], [1, 16]], 0, 0, allow_small_or_imprecise_dtypes=True))
         for i, h in enumerate(team):
             g.wait_ge(T.sem["l_t%d" % i], 16)
-            same([h], tq[i], S.a_tabq, onchip)
+            same([h], tq[i], tq[i], S.a_tabq, onchip)
         c2 = phase()
         wait(V, c0, c1)
         on(c2, V.tensor_scalar(T.PJ[:, 0:1], T.PI[:], 3, None, A.arith_shift_right))
@@ -158,13 +174,13 @@ def rank_program(g, core, T, topo):
             on(p, V.tensor_scalar(T.OHA[:, 48 + j:112:16], T.W1[:, 0:4], float(j), None, A.is_equal))
         on(p2, V.tensor_scalar(T.W2[:, 0:4], T.W1[:, 0:4], 1, None, A.bitwise_and))
         on(p2, V.tensor_scalar(T.W3[:, 0:4], T.W1[:, 0:4], 1, None, A.arith_shift_right))
-        fin = ranks(4, N, T.OHA, T.P0, T.RA, [c0, c1, p])
+        pm = count(4, N, T.OHA, T.P0, [c0, c1, p])
         wait(V, p2)
         p3, p4 = phase(), phase()
         on(p4, V.tensor_copy(T.F2[:, 0:4], T.W3[:, 0:4]))
         s, o = (-64.0, 63.0) if par else (64.0, -1.0)
         on(p3, V.tensor_scalar(T.F1[:, 0:4], T.W2[:, 0:4], s, o, A.mult, A.add))
-        pr = fin()
+        pr = ranks(4, N, T.OHA, T.P0, T.RA, pm)
         wait(V, pr, p3)
         p = phase()
         on(p, V.tensor_tensor(T.F3[:, 0:4], T.F1[:, 0:4], T.RA[:], A.add))
@@ -180,7 +196,7 @@ def rank_program(g, core, T, topo):
         wait(V, pt)
         pt2 = phase()
         on(pt2, V.tensor_copy(T.PP[:], T.P1[:]))
-        V.wait_ge(S.a_rel, len(onchip))
+        V.wait_ge(S.a_rel, len(common(teams[(rank + 1) % N])))
         wait(V, pq)
         p = phase()
         on(p, V.tensor_scalar(T.W1[:], T.LM[:], 13, None, A.arith_shift_right))
@@ -189,8 +205,8 @@ def rank_program(g, core, T, topo):
         for j in range(N):
             on(p, V.tensor_scalar(T.OHB[:, 112 + j:240:16], T.W1[:], float(16 + j), None, A.is_equal))
         on(p2, V.tensor_scalar(T.F1[:], T.W1[:], 64.0, -1025.0, A.mult, A.add))
-        fin = ranks(8, N, T.OHB, T.P2, T.RB, [p])
-        pr = fin()
+        pm = count(8, N, T.OHB, T.P2, [p])
+        pr = ranks(8, N, T.OHB, T.P2, T.RB, pm)
         wait(V, pr, p2)
         p = phase()
         on(p, V.tensor_tensor(T.F2[:], T.F1[:], T.RB[:], A.add))
@@ -239,38 +255,39 @@ def rank_program(g, core, T, topo):
     u = me % K
     par = u & 1
     served = [r for r in range(N) if _kk(r, me) == k]
-    classes = [K * k + j for j in range(K)]
+    classes = [m for m in range(N) if _ks(me, m) == k]
     to = [teams[m][_kk(me, m)] for m in classes]
     onchip = _bits(topo.mask(core, T.cores[me]))
-    off = _bits(topo.mask(core, teams[(me + 1) % N][0]))
+    off = common(teams[(me + 1) % N])
     high = [b for b in onchip if b not in off]
-    nq, nh = len(onchip) // K, len(onchip) // 2
+    nq = len(onchip) // K
+    fwd = [high if i == 0 else onchip for i in range(K)]
 
     c0 = phase()
     on(c0, V.memset(T.ONB[:], 1.0))
+    on(c0, V.memset(T.SHB[:], 1.0))
     on(c0, V.memset(T.OHA[:, 0:12], 0.0))
     on(c0, V.memset(T.OHB[:, 0:28], 0.0))
     on(c0, V.memset(T.ONF[:], 1.0))
     on(c0, V.memset(T.BIG[0:1, :], 131072.0))
-    on(c0, V.memset(T.T8[0:16, :], 1.0))
     c1, c1b, c1c = phase(), phase(), phase()
-    on(c1, g.iota(T.DI[:], [[-1, 128]], 128, 1))
+    on(c1, g.iota(T.DA[:], [[-1, 128]], 128, 1))
     on(c1, g.iota(T.PI[:], [[0, 1]], 0, 1))
     on(c1, g.iota(T.IO1[:], [[1, 64]], 1, 0, allow_small_or_imprecise_dtypes=True))
     wait(g, c0)
     on(c1b, g.affine_select(T.TRI[:], T.ONB[:], [[1, 128]], A.is_ge, 0.0, 0, -1))
     on(c1c, g.affine_select(T.IDF[:], T.ONF[:], [[-1, 128]], A.is_equal, 0.0, 0, 1))
     on(c1c, g.iota(T.IOK[:], [[1, 128]], 128, 0, allow_small_or_imprecise_dtypes=True))
-    on(c1c, g.affine_select(T.T8[0:16, :], T.T8[0:16, :], [[-16, 8], [1, 128]], A.is_equal, 0.0, 0, -1))
+    on(c1c, g.affine_select(T.SHB[:], T.SHB[:], [[-64, 2], [1, 128]], A.is_equal, 0.0, 0, -1))
     wait(V, c0, c1)
     c2 = phase()
-    on(c2, V.tensor_scalar(T.DA[:], T.DI[:], 15, None, A.bitwise_and))
+    on(c2, V.tensor_scalar(T.DA[:], T.DA[:], 15, None, A.bitwise_and))
     on(c2, V.tensor_scalar(T.PJ[:, 0:1], T.PI[:], 4, None, A.arith_shift_right))
     wait(V, c2)
     c3 = phase()
-    on(c3, V.tensor_scalar(T.SEF[:], T.DA[:], 0.0, None, A.is_equal))
     on(c3, V.tensor_scalar(T.SE1[:], T.DA[:], 0.0, None, A.is_equal))
     on(c3, V.tensor_scalar(T.SE2[:], T.DA[:], 0.0, 128.0, A.is_equal, A.mult))
+    on(c3, V.tensor_scalar(T.SE3[:], T.DA[:], 0.0, 32.0, A.is_equal, A.mult))
     for h in range(4):
         on(c3, V.tensor_scalar(T.MKH[:, h:h + 1], T.PJ[:, 0:1], float(h), None, A.is_equal))
     wait(V, c3)
@@ -280,71 +297,67 @@ def rank_program(g, core, T, topo):
     for b in range(2):
         on(cg, TE.matmul(PG[b][:, 0:128], T.ONF[0:1, :], T.BIG[0:1, :], True, False))
 
-    def wrap(PSP, parts, Ebuf, sels, PSW, out, pre, selfs, landing):
-        n = 4 * parts
+    def wrap(PSP, sels, PSW, pre):
         wait(V, pre)
         pe = phase()
         for h in range(4):
-            on(pe, V.tensor_scalar(Ebuf[0:64, h:4 * n:4], PSP[0:64, 0:n], T.MKH[0:64, h:h + 1], None, A.mult))
+            on(pe, V.tensor_scalar(T.EB[0:64, h:32:4], PSP[0:64, 0:8], T.MKH[0:64, h:h + 1], None, A.mult))
         wait(TE, c3, pe)
         pm = phase()
-        for i in range(parts):
-            on(pm, TE.matmul(PSW[:, 0:16], sels[i][0:64, :], Ebuf[0:64, 16 * i:16 * i + 16], i == 0, i == parts - 1))
-        wait(V, pm)
-        po, ps = phase(), phase()
-        on(po, V.tensor_copy(out[:], PSW[:, 0:16]))
-        for j, col in selfs:
-            on(ps, V.tensor_copy(landing[:, col:col + 4], PSW[:, 4 * j:4 * j + 4]))
-        return po, ps
+        for i in range(2):
+            on(pm, TE.matmul(PSW[:, 0:16], sels[i][0:64, :], T.EB[0:64, 16 * i:16 * i + 16], i == 0, i == 1))
+        return pm
 
-    V.wait_ge(S.a_idx, nh)
-    p = phase()
-    on(p, V.tensor_scalar(T.W1[:, 0:4], T.IX[:], 17, None, A.arith_shift_right))
-    on(p, V.tensor_scalar(T.W2[:, 0:4], T.IX[:], 15, None, A.bitwise_and))
-    on(p, V.tensor_scalar(T.W3[:, 0:4], T.IX[:], 4, 8191, A.arith_shift_right, A.bitwise_and))
-    wait(V, p)
+    for i in range(K):
+        q = g.sync if i < 2 else g.scalar
+        if i % 2 == 0:
+            q.wait_ge(S.a_h1, K * len(off))
+        blk = 4 * (i ^ (me & 1))
+        q.dma_start(T.RAW[:, blk:blk + 4], T.IXL[i]).then_inc(S.l_in, 16)
+    V.wait_ge(S.l_in, 16 * K)
+    R = [T.RI[:, 16 * i:16 * i + 16] for i in range(5)]
     p, p2 = phase(), phase()
     for j in range(K):
-        on(p, V.tensor_scalar(T.OHA[:, 12 + j:28:4], T.W1[:, 0:4], float(classes[j]), None, A.is_equal))
-    on(p2, V.tensor_scalar(T.F1[:, 0:4], T.W2[:, 0:4], 8192.0, 131072.0, A.mult, A.add))
-    fin = ranks(4, K, T.OHA, T.P0, T.RA, [c1b, p])
-    wait(V, p2)
-    p2 = phase()
-    on(p2, V.tensor_tensor(T.F2[:, 0:4], T.F1[:, 0:4], T.W3[:, 0:4], A.add))
-    wait(V, p, p2)
-    p2 = phase()
-    for j in range(K):
-        on(p2, V.tensor_tensor(T.OV[:, j:16:4], T.OHA[:, 12 + j:28:4], T.F2[:, 0:4], A.mult))
-    pr = fin()
-    wait(V, pr)
-    pl = [phase(), phase()]
-    for c in range(4):
-        on(pl[c // 2], V.tensor_scalar(T.LF[:, 64 * c:64 * c + 64], T.IO1[:], T.RA[:, c:c + 1], None, A.is_equal))
-    wait(TE, p2)
-    pm = phase()
-    for c in range(4):
-        if c % 2 == 0:
-            wait(TE, pl[c // 2])
-        on(pm, TE.matmul(T.P1[0:64, 0:4], T.LF[:, 64 * c:64 * c + 64], T.OV[:, 4 * c:4 * c + 4], c == 0, c == 3))
-    land = [4 * (u ^ (m & 1)) for m in classes]
-    po, ps1 = wrap(T.P1, 1, T.EF, [T.SEF], T.P2, T.MS1, pm, [(j, land[j]) for j in range(K) if to[j] == core], T.H1L)
-    g.wait_ge(S.a_mpq, nq)
-    same(others, T.MP[:, 256 * k:256 * k + 256], S.a_mpo, onchip)
-    wait(g, po)
-    each([(to[j], T.H1L[:, land[j]:land[j] + 4], T.MS1[:, 4 * j:4 * j + 4]) for j in range(K) if to[j] != core], S.a_h1)
-
-    n1 = len([r for r in served if teams[r][me // K] != core])
-    V.wait_ge(S.a_h1, 2 * n1)
-    wait(V, ps1)
-    p, pb = phase(), phase()
-    on(p, V.tensor_scalar(T.KA[:], T.H1L[:], 1023, None, A.bitwise_and))
-    on(pb, V.tensor_scalar(T.KB[:], T.H1L[:], 10, None, A.arith_shift_right))
+        on(p, V.tensor_scalar(T.RI[:, 4 * j:4 * j + 4], T.RAW[:, 4 * j:4 * j + 4], 17, None, A.arith_shift_right))
+    on(p2, V.tensor_scalar(R[1], T.RAW[:], 9, 31, A.arith_shift_right, A.bitwise_and))
+    on(p2, V.tensor_scalar(R[2], T.RAW[:], 4, 31, A.arith_shift_right, A.bitwise_and))
+    on(p2, V.tensor_scalar(R[3], T.RAW[:], 15, None, A.bitwise_and))
+    on(p2, V.tensor_scalar(R[4], T.RAW[:], 14, 7, A.arith_shift_right, A.bitwise_and))
     wait(V, p)
     p = phase()
-    on(p, V.tensor_copy(T.OF1[:, 0:16], T.KA[:]))
-    wait(V, pb)
+    for j in range(K):
+        on(p, V.tensor_scalar(T.OHA[:, 12 + j:28:4], T.RI[:, 4 * j:4 * j + 4], float(me), None, A.is_equal))
+    pm = count(4, K, T.OHA, T.P0, [c1b, p])
+    wait(V, p2)
+    pk, p2 = phase(), phase()
+    on(p2, V.tensor_scalar(T.FA[:], R[3], 8.0, 128.0, A.mult, A.add))
+    on(pk, V.tensor_copy(T.PB[:, 0:48:3], R[1]))
+    on(pk, V.tensor_copy(T.PB[:, 1:48:3], R[2]))
+    wait(V, p2)
+    on(pk, V.tensor_tensor(T.PB[:, 2:48:3], T.FA[:], R[4], A.add))
+    wait(V, p)
+    pr = own(4, K, T.OHA, T.P0, pm)
+    wait(V, pr)
+    pl = [phase() for _ in range(K)]
+    for n in range(16):
+        j, c = n // 4, n % 4
+        on(pl[j], V.tensor_scalar(T.LB[:, 64 * n:64 * n + 64], T.IO1[:], T.ZA[:, 4 * c + j:4 * c + j + 1], None, A.is_equal))
+    wait(TE, pk)
+    pm = phase()
+    for n in range(16):
+        j, c = n // 4, n % 4
+        if c == 0:
+            wait(TE, pl[j])
+        on(pm, TE.matmul(T.P1[0:64, j:12:4], T.LB[:, 64 * n:64 * n + 64], T.PB[:, 3 * n:3 * n + 3], c == 0, c == 3))
+    pw = wrap(T.P1, [T.SE3, T.SE1], T.P2, pm)
     pb = phase()
-    on(pb, V.tensor_copy(T.KC[:], T.KB[:]))
+    on(pb, V.tensor_copy(T.KC[0:64, :], T.P1[0:64, 8:12]))
+    wait(V, pw)
+    p = phase()
+    on(p, V.tensor_copy(T.OF1[:, 0:16], T.P2[:, 0:16]))
+    g.wait_ge(S.a_mpq, nq)
+    same(others, T.MP[:, 256 * k:256 * k + 256], T.MP[:, 256 * k:256 * k + 256], S.a_mpo, onchip)
+
     V.wait_ge(S.a_mpq, nq)
     V.wait_ge(S.a_mpo, (K - 1) * len(onchip))
     wait(V, p)
@@ -353,8 +366,8 @@ def rank_program(g, core, T, topo):
         on(pg[b], V.tensor_copy(T.GG[:, 128 * b:128 * b + 128], T.MP[:].indirect(T.OF1[:, 8 * b:8 * b + 8])))
     wait(TE, c1c, pb)
     pk = phase()
-    for n in range(8):
-        on(pk, TE.matmul(T.P3[:, 0:2], T.T8[0:16, 128 * n:128 * n + 128], T.KC[0:16, n:16:8], n == 0, n == 7))
+    for n in range(2):
+        on(pk, TE.matmul(T.P3[:, 0:2], T.SHB[0:64, 128 * n:128 * n + 128], T.KC[0:64, n:4:2], n == 0, n == 1))
     pgt = [phase(), phase()]
     wait(TE, cg)
     for b in range(2):
@@ -379,10 +392,16 @@ def rank_program(g, core, T, topo):
         if teams[r][0] == core:
             wait(V, pv)
             on(ps2, V.tensor_copy(lv, T.VV[:, blk[r]:blk[r] + 1]))
+
+    def table():
+        g.wait_ge(S.a_tabq, len(onchip))
+        same(others, T.TAB[:, 2048 * k:2048 * k + 2048], T.TAB[:, 2048 * k:2048 * k + 2048], S.a_tabo, fwd[k])
+    if k == 0:
+        table()
     wait(g, pv)
     each([(teams[r][0], lv, T.VV[:, blk[r]:blk[r] + 1]) for r in served if teams[r][0] != core], S.a_h2)
-    g.wait_ge(S.a_tabq, len(onchip))
-    same(others, T.TAB[:, 2048 * k:2048 * k + 2048], S.a_tabo, high)
+    if k:
+        table()
 
     if k == 0:
         n2 = len([m for m in range(N) if teams[m][_kk(me, m)] != core])
@@ -392,10 +411,10 @@ def rank_program(g, core, T, topo):
         on(p, V.tensor_copy(T.LM[0:64, :], T.LV[0:64, 4 * par:64:8]))
         on(p, V.tensor_copy(T.LM[64:128, :], T.LV[64:128, 4 * (1 - par):64:8]))
         wait(g, p)
-        same(others + [T.cores[me]], T.LM[:], S.a_rel, onchip)
+        same(others + [T.cores[me]], T.LM[:], T.LM[:], S.a_rel, off)
         wait(V, p)
     else:
-        V.wait_ge(S.a_rel, len(onchip))
+        V.wait_ge(S.a_rel, len(off))
 
     p = phase()
     on(p, V.tensor_scalar(T.W1[:], T.LM[:], 13, None, A.arith_shift_right))
@@ -405,13 +424,13 @@ def rank_program(g, core, T, topo):
     p = phase()
     for j in range(K):
         on(p, V.tensor_scalar(T.OHB[:, 28 + j:60:4], T.W1[:], float(16 + classes[j]), None, A.is_equal))
-    fin = ranks(8, K, T.OHB, T.P0, T.RB, [p])
+    pm = count(8, K, T.OHB, T.P0, [p])
     wait(V, p)
     p2 = phase()
     for j in range(K):
         on(p2, V.tensor_tensor(T.OW[:, j:64:8], T.OHB[:, 28 + j:60:4], T.W2[:], A.mult))
         on(p2, V.tensor_tensor(T.OW[:, 4 + j:64:8], T.OHB[:, 28 + j:60:4], T.W3[:], A.mult))
-    pr = fin()
+    pr = ranks(8, K, T.OHB, T.P0, T.RB, pm)
     wait(V, pr)
     pl = [phase() for _ in range(4)]
     for c in range(8):
@@ -422,11 +441,17 @@ def rank_program(g, core, T, topo):
         if c % 2 == 0:
             wait(TE, pl[c // 2])
         on(pm, TE.matmul(T.P1[0:64, 0:8], T.LB[:, 64 * c:64 * c + 64], T.OW[:, 8 * c:8 * c + 8], c == 0, c == 7))
-    po, ps3 = wrap(T.P1, 2, T.EB, [T.SE2, T.SE1], T.P2, T.MS3, pm, [(j, 4 * u) for j in range(K) if to[j] == core], T.H3L)
+    pw = wrap(T.P1, [T.SE2, T.SE1], T.P2, pm)
+    wait(V, pw)
+    po, ps3 = phase(), phase()
+    on(po, V.tensor_copy(T.MS3[:], T.P2[:, 0:16]))
+    for j in range(K):
+        if to[j] == core:
+            on(ps3, V.tensor_copy(T.H3L[:, 4 * u:4 * u + 4], T.P2[:, 4 * j:4 * j + 4]))
     wait(g, po)
     each([(to[j], T.H3L[:, 4 * u:4 * u + 4], T.MS3[:, 4 * j:4 * j + 4]) for j in range(K) if to[j] != core], S.a_h3)
 
-    V.wait_ge(S.a_h3, 2 * n1)
+    V.wait_ge(S.a_h3, 2 * len([r for r in served if teams[r][_ks(r, me)] != core]))
     wait(V, ps3)
     p = phase()
     on(p, V.tensor_copy(T.OF3[:], T.H3L[:]))
@@ -434,7 +459,7 @@ def rank_program(g, core, T, topo):
     for b, q in enumerate([V, g.scalar]):
         wait(q, p)
         q.wait_ge(S.a_tabq, len(onchip))
-        q.wait_ge(S.a_tabo, (K - 1) * len(high))
+        q.wait_ge(S.a_tabo, sum(len(fwd[i]) for i in range(K) if i != k))
         o, i = T.RES[:, 128 * b:128 * b + 128], T.TAB[:].indirect(T.OF3[:, 8 * b:8 * b + 8])
         on(pc[b], V.tensor_copy(o, i) if b == 0 else g.scalar.activation(o, i, AF.Copy))
     wait(g, pc[0], pc[1])

@@ -6,7 +6,7 @@ NCORES = 256
 I32, F32, B16, U16 = "int32", "float32", "bfloat16", "uint16"
 _SB = {
     "IX": (4, I32), "MP": (1024, I32), "TAB": (8192, B16), "LV": (64, F32), "VV": (2, F32),
-    "LM": (8, I32), "H3L": (16, I32), "MS3": (16, I32), "RES": (512, B16), "LAND": (1024, B16),
+    "LM": (8, I32), "H3L": (16, U16), "MS3": (16, U16), "RES": (512, B16), "LAND": (1024, B16), "COL": (256, B16),
     "ONB": (128, B16), "TRI": (128, B16), "IO1": (64, B16), "IOK": (128, B16), "IDF": (128, F32), "SHB": (256, B16),
     "DA": (128, I32), "SE1": (128, B16), "SE2": (128, B16), "SE3": (128, B16), "SEF": (128, F32),
     "PI": (1, I32), "PJ": (2, I32), "MKH": (8, F32), "ONF": (128, F32), "BIG": (128, F32),
@@ -14,26 +14,29 @@ _SB = {
     "W1": (8, I32), "W2": (8, I32), "W3": (8, I32), "F1": (8, F32), "F2": (8, F32), "F3": (8, F32), "OHA": (112, B16),
     "OHB": (240, B16), "ZA": (128, F32), "ZB": (64, F32), "ZC": (32, F32), "ZD": (16, F32), "RA": (4, F32), "RB": (8, F32),
     "OW": (64, B16), "LF": (512, F32), "LB": (1024, B16), "EF": (32, F32), "EB": (32, B16),
-    "OF1": (32, U16), "OF3": (16, U16), "GG": (256, F32), "MM": (256, F32), "PP": (512, F32),
+    "OF1": (32, U16), "GG": (256, F32), "MM": (256, F32), "PP": (512, F32),
 }
 SCRATCH = {n: ("sbuf", [128, w], d) for n, (w, d) in _SB.items()}
 SCRATCH.update({"P%d" % i: ("psum", [128, 512], F32) for i in range(6)})
 SCRATCH["IXD"] = ("dram", [128, 4], I32)
 SCRATCH["IXL"] = ("dram", [K, 128, 4], I32)
-SEMAPHORES = (["a_mpq", "a_mpo", "a_tabq", "a_tabo", "a_h1", "a_h2", "a_rel", "a_h3", "a_h4", "loc",
-               "l_ixd", "l_idx", "l_mp", "l_y", "l_in"] + ["l_t%d" % i for i in range(K)] + ["c%d" % i for i in range(90)])
+PIECES = [(1, 0, 2048, 0), (2, 2048, 2048, 1), (3, 4096, 2048, 2), (1, 6144, 1024, 3), (2, 7168, 1024, 3)]
+SEMAPHORES = (["a_mpq", "a_mpo", "a_tabo", "a_h1", "a_h2", "a_rel", "a_h3", "a_h4", "loc", "go",
+               "l_ixd", "l_idx", "l_mp", "l_y", "l_in"] + ["a_p%d" % i for i in range(len(PIECES))]
+              + ["l_t%d" % i for i in range(4)] + ["c%d" % i for i in range(90)])
 _CACHE = {}
 
 
 def _teams(T, topo):
     if "t" not in _CACHE:
-        out = []
+        helpers, servers = [], []
         for c in T.cores:
             chip = [d for d in range(NCORES) if d != c and topo.host(d) == topo.host(c) and topo.chip(d) == topo.chip(c)]
             near = [d for d in chip if topo.die(d) == topo.die(c)]
             far = [d for d in chip if topo.die(d) != topo.die(c)]
-            out.append([near[0], far[0], near[1], far[1]])
-        _CACHE["t"] = out
+            helpers.append([near[0], far[0], near[1], far[1]])
+            servers.append([c, near[2], far[2], far[3]])
+        _CACHE["t"] = (helpers, servers)
     return _CACHE["t"]
 
 
@@ -45,6 +48,10 @@ def _ks(r, m):
     return (m // K + r) % K
 
 
+def _kt(r, m):
+    return (r // K - m // K + 1 + m % 3) % K
+
+
 def _bits(mask):
     return [i for i in range(16) if (mask >> i) & 1]
 
@@ -54,7 +61,7 @@ def _mask(bits):
 
 
 def rank_program(g, core, T, topo):
-    teams = _teams(T, topo)
+    teams, servers = _teams(T, topo)
     rank = T.rank_of(core)
     S, V, TE = T.sem, g.vector, g.tensor
     used, loc = [0], [0]
@@ -93,6 +100,17 @@ def rank_program(g, core, T, topo):
                                               srcs=[in_], dsts=[out for _d in dests])], local_sem=S.loc)
         loc[0] += len(bits)
 
+    def tab(i):
+        return T.TAB[:, PIECES[i][1]:PIECES[i][1] + PIECES[i][2]]
+
+    def shares(onchip):
+        out = []
+        for _s, _c, _w, load in PIECES:
+            same_load = [i for i in range(len(PIECES)) if PIECES[i][3] == load]
+            n, j = len(onchip) // len(same_load), len([1 for i in same_load if i < len(out)])
+            out.append(onchip[n * j:n * j + n])
+        return out
+
     def count(C, J, OH, PS, pre):
         z, w = (C - 1) * J, C * J
         pm = phase()
@@ -125,34 +143,42 @@ def rank_program(g, core, T, topo):
         onchip = _bits(topo.mask(core, team[0]))
         nq = len(onchip) // K
         g.sync.dma_start(T.IXD[:], T.idx[:]).then_inc(S.l_ixd, 16)
-        g.sync.dma_start(T.IX[:], T.idx[:]).then_inc(S.l_idx, 16)
         g.scalar.dma_start(T.MP[:], T.mp[:]).then_inc(S.l_mp, 16)
-        g.sync.wait_ge(S.l_mp, 16)
-        tq = [T.TAB[:, 2048 * i:2048 * i + 2048] for i in range(K)]
-        for i in range(K):
-            g.sync.dma_start(tq[i], T.tab[:, 2048 * i:2048 * i + 2048]).then_inc(T.sem["l_t%d" % i], 16)
+        g.sync.dma_start(T.IX[:], T.idx[:]).then_inc(S.l_idx, 16)
+        g.scalar.dma_start(T.TAB[:, 0:1024], T.tab[:, 0:1024]).then_inc(S.l_t0, 16)
+        g.sync.wait_ge(S.go, 1)
+        g.sync.dma_start(T.TAB[:, 1024:2048], T.tab[:, 1024:2048]).then_inc(S.l_t0, 16)
+        for i in range(1, 4):
+            g.sync.dma_start(T.TAB[:, 2048 * i:2048 * i + 2048], T.tab[:, 2048 * i:2048 * i + 2048]).then_inc(T.sem["l_t%d" % i], 16)
+        tload = [32, 16, 16, 16]
         c0, c1 = phase(), phase()
         on(c0, V.memset(T.ONB[:], 1.0))
         on(c0, V.memset(T.ONF[:], 1.0))
         on(c0, V.memset(T.OHA[:, 0:48], 0.0))
         on(c0, V.memset(T.OHB[:, 0:112], 0.0))
-        on(c1, g.iota(T.IOK[:], [[1, 128]], 0, 0, allow_small_or_imprecise_dtypes=True))
-        on(c1, g.iota(T.PI[:], [[0, 1]], 0, 1))
-        on(c1, g.iota(T.BIG[:], [[0, 8], [1, 16]], 0, 0, allow_small_or_imprecise_dtypes=True))
         g.wait_ge(S.l_ixd, 16)
         where = [teams[m][_kk(rank, m)] for m in range(N)]
-        same(where, T.IXL[rank % K], T.IXD[:], S.a_h1, common(where))
+        same(where, T.IXL[rank % K], T.IXD[:], S.a_h1, common(where)[:K])
         g.wait_ge(S.l_mp, 16)
         g.remote_dma_fused([RemoteDMATransfer(dst_ids=[dst(h)], dma_engine_mask=_mask(onchip[nq * i:nq * i + nq]), remote_sem=S.a_mpq,
                                               src=T.MP[:, 256 * i:256 * i + 256], dst=T.MP[:, 256 * i:256 * i + 256])
                             for i, h in enumerate(team)], local_sem=S.loc)
         loc[0] += len(onchip)
+        g.sem_inc(S.go, 1)
+        on(c1, g.iota(T.IOK[:], [[1, 128]], 0, 0, allow_small_or_imprecise_dtypes=True))
+        on(c1, g.iota(T.PI[:], [[0, 1]], 0, 1))
+        on(c1, g.iota(T.BIG[:], [[0, 8], [1, 16]], 0, 0, allow_small_or_imprecise_dtypes=True))
         wait(g, c0)
         on(c1, g.affine_select(T.TRI[:], T.ONB[:], [[1, 128]], A.is_ge, 0.0, 0, -1))
         on(c1, g.affine_select(T.IDF[:], T.ONF[:], [[-1, 128]], A.is_equal, 0.0, 0, 1))
-        for i, h in enumerate(team):
-            g.wait_ge(T.sem["l_t%d" % i], 16)
-            same([h], tq[i], tq[i], S.a_tabq, onchip)
+        sh = shares(onchip)
+        for load in range(4):
+            g.wait_ge(T.sem["l_t%d" % load], tload[load])
+            ps = [i for i in range(len(PIECES)) if PIECES[i][3] == load]
+            g.remote_dma_fused([RemoteDMATransfer(dst_ids=[dst(servers[rank][PIECES[i][0]])], dma_engine_mask=_mask(sh[i]),
+                                                  remote_sem=T.sem["a_p%d" % i], src=tab(i), dst=tab(i)) for i in ps],
+                               local_sem=S.loc)
+            loc[0] += sum(len(sh[i]) for i in ps)
         c2 = phase()
         wait(V, c0, c1)
         on(c2, V.tensor_scalar(T.PJ[:, 0:1], T.PI[:], 3, None, A.arith_shift_right))
@@ -196,7 +222,15 @@ def rank_program(g, core, T, topo):
         wait(V, pt)
         pt2 = phase()
         on(pt2, V.tensor_copy(T.PP[:], T.P1[:]))
-        V.wait_ge(S.a_rel, len(common(teams[(rank + 1) % N])))
+        served = [r for r in range(N) if _kt(r, rank) == 0]
+        for i in range(4):
+            g.scalar.wait_ge(T.sem["l_t%d" % i], tload[i])
+        g.scalar.wait_ge(S.a_h3, 2 * len(served))
+        pc = phase()
+        on(pc, g.scalar.activation(T.COL[:], T.TAB[:].indirect(T.H3L[:]), AF.Copy))
+        wait(g, pc)
+        each([(T.cores[r], T.LAND[:, 64 * rank:64 * rank + 64], T.COL[:, 64 * (r % K):64 * (r % K) + 64]) for r in served], S.a_h4)
+        V.wait_ge(S.a_rel, len(onchip))
         wait(V, pq)
         p = phase()
         on(p, V.tensor_scalar(T.W1[:], T.LM[:], 13, None, A.arith_shift_right))
@@ -245,6 +279,32 @@ def rank_program(g, core, T, topo):
         g.wait_ge(S.loc, loc[0])
         return
 
+    own_server = [r for r in range(N) if core in servers[r]]
+    if own_server:
+        me = own_server[0]
+        mates = servers[me]
+        s = mates.index(core)
+        served = [r for r in range(N) if _kt(r, me) == s]
+        onchip = _bits(topo.mask(core, T.cores[me]))
+        sh = shares(onchip)
+        others = [d for d in mates if d != core and d != T.cores[me]]
+        mine = [i for i in range(len(PIECES)) if PIECES[i][0] == s]
+        for i in mine:
+            g.wait_ge(T.sem["a_p%d" % i], len(sh[i]))
+            same(others, tab(i), tab(i), S.a_tabo, onchip)
+        pc = [phase(), phase()]
+        for b, q in enumerate([V, g.scalar]):
+            for i in mine:
+                q.wait_ge(T.sem["a_p%d" % i], len(sh[i]))
+            q.wait_ge(S.a_tabo, len(onchip) * (len(PIECES) - len(mine)))
+            q.wait_ge(S.a_h3, 2 * len(served))
+            o, i = T.COL[:, 128 * b:128 * b + 128], T.TAB[:].indirect(T.H3L[:, 8 * b:8 * b + 8])
+            on(pc[b], V.tensor_copy(o, i) if b == 0 else g.scalar.activation(o, i, AF.Copy))
+        wait(g, pc[0], pc[1])
+        each([(T.cores[r], T.LAND[:, 64 * me:64 * me + 64], T.COL[:, 64 * (r % K):64 * (r % K) + 64]) for r in served], S.a_h4)
+        g.wait_ge(S.loc, loc[0])
+        return
+
     mine = [r for r in range(N) if core in teams[r]]
     if not mine:
         return
@@ -256,12 +316,9 @@ def rank_program(g, core, T, topo):
     par = u & 1
     served = [r for r in range(N) if _kk(r, me) == k]
     classes = [m for m in range(N) if _ks(me, m) == k]
-    to = [teams[m][_kk(me, m)] for m in classes]
+    to = [servers[m][_kt(me, m)] for m in classes]
     onchip = _bits(topo.mask(core, T.cores[me]))
-    off = common(teams[(me + 1) % N])
-    high = [b for b in onchip if b not in off]
     nq = len(onchip) // K
-    fwd = [high if i == 0 else onchip for i in range(K)]
 
     c0 = phase()
     on(c0, V.memset(T.ONB[:], 1.0))
@@ -311,22 +368,21 @@ def rank_program(g, core, T, topo):
     for i in range(K):
         q = g.sync if i < 2 else g.scalar
         if i % 2 == 0:
-            q.wait_ge(S.a_h1, K * len(off))
+            q.wait_ge(S.a_h1, K * K)
         blk = 4 * (i ^ (me & 1))
         q.dma_start(T.RAW[:, blk:blk + 4], T.IXL[i]).then_inc(S.l_in, 16)
     V.wait_ge(S.l_in, 16 * K)
     R = [T.RI[:, 16 * i:16 * i + 16] for i in range(5)]
     p, p2 = phase(), phase()
-    for j in range(K):
-        on(p, V.tensor_scalar(T.RI[:, 4 * j:4 * j + 4], T.RAW[:, 4 * j:4 * j + 4], 17, None, A.arith_shift_right))
+    on(p, V.tensor_scalar(R[0], T.RAW[:], 17, None, A.arith_shift_right))
     on(p2, V.tensor_scalar(R[1], T.RAW[:], 9, 31, A.arith_shift_right, A.bitwise_and))
-    on(p2, V.tensor_scalar(R[2], T.RAW[:], 4, 31, A.arith_shift_right, A.bitwise_and))
-    on(p2, V.tensor_scalar(R[3], T.RAW[:], 15, None, A.bitwise_and))
-    on(p2, V.tensor_scalar(R[4], T.RAW[:], 14, 7, A.arith_shift_right, A.bitwise_and))
     wait(V, p)
     p = phase()
     for j in range(K):
         on(p, V.tensor_scalar(T.OHA[:, 12 + j:28:4], T.RI[:, 4 * j:4 * j + 4], float(me), None, A.is_equal))
+    on(p2, V.tensor_scalar(R[2], T.RAW[:], 4, 31, A.arith_shift_right, A.bitwise_and))
+    on(p2, V.tensor_scalar(R[3], T.RAW[:], 15, None, A.bitwise_and))
+    on(p2, V.tensor_scalar(R[4], T.RAW[:], 14, 7, A.arith_shift_right, A.bitwise_and))
     pm = count(4, K, T.OHA, T.P0, [c1b, p])
     wait(V, p2)
     pk, p2 = phase(), phase()
@@ -392,16 +448,8 @@ def rank_program(g, core, T, topo):
         if teams[r][0] == core:
             wait(V, pv)
             on(ps2, V.tensor_copy(lv, T.VV[:, blk[r]:blk[r] + 1]))
-
-    def table():
-        g.wait_ge(S.a_tabq, len(onchip))
-        same(others, T.TAB[:, 2048 * k:2048 * k + 2048], T.TAB[:, 2048 * k:2048 * k + 2048], S.a_tabo, fwd[k])
-    if k == 0:
-        table()
     wait(g, pv)
     each([(teams[r][0], lv, T.VV[:, blk[r]:blk[r] + 1]) for r in served if teams[r][0] != core], S.a_h2)
-    if k:
-        table()
 
     if k == 0:
         n2 = len([m for m in range(N) if teams[m][_kk(me, m)] != core])
@@ -411,21 +459,21 @@ def rank_program(g, core, T, topo):
         on(p, V.tensor_copy(T.LM[0:64, :], T.LV[0:64, 4 * par:64:8]))
         on(p, V.tensor_copy(T.LM[64:128, :], T.LV[64:128, 4 * (1 - par):64:8]))
         wait(g, p)
-        same(others + [T.cores[me]], T.LM[:], T.LM[:], S.a_rel, off)
+        same(others + [T.cores[me]], T.LM[:], T.LM[:], S.a_rel, onchip)
         wait(V, p)
     else:
-        V.wait_ge(S.a_rel, len(off))
+        V.wait_ge(S.a_rel, len(onchip))
 
-    p = phase()
+    p, p2 = phase(), phase()
     on(p, V.tensor_scalar(T.W1[:], T.LM[:], 13, None, A.arith_shift_right))
-    on(p, V.tensor_scalar(T.W2[:], T.LM[:], 7, 63, A.arith_shift_right, A.bitwise_and))
-    on(p, V.tensor_scalar(T.W3[:], T.LM[:], 127, None, A.bitwise_and))
+    on(p2, V.tensor_scalar(T.W2[:], T.LM[:], 7, 63, A.arith_shift_right, A.bitwise_and))
     wait(V, p)
     p = phase()
     for j in range(K):
         on(p, V.tensor_scalar(T.OHB[:, 28 + j:60:4], T.W1[:], float(16 + classes[j]), None, A.is_equal))
+    on(p2, V.tensor_scalar(T.W3[:], T.LM[:], 127, None, A.bitwise_and))
     pm = count(8, K, T.OHB, T.P0, [p])
-    wait(V, p)
+    wait(V, p, p2)
     p2 = phase()
     for j in range(K):
         on(p2, V.tensor_tensor(T.OW[:, j:64:8], T.OHB[:, 28 + j:60:4], T.W2[:], A.mult))
@@ -443,25 +491,8 @@ def rank_program(g, core, T, topo):
         on(pm, TE.matmul(T.P1[0:64, 0:8], T.LB[:, 64 * c:64 * c + 64], T.OW[:, 8 * c:8 * c + 8], c == 0, c == 7))
     pw = wrap(T.P1, [T.SE2, T.SE1], T.P2, pm)
     wait(V, pw)
-    po, ps3 = phase(), phase()
+    po = phase()
     on(po, V.tensor_copy(T.MS3[:], T.P2[:, 0:16]))
-    for j in range(K):
-        if to[j] == core:
-            on(ps3, V.tensor_copy(T.H3L[:, 4 * u:4 * u + 4], T.P2[:, 4 * j:4 * j + 4]))
     wait(g, po)
-    each([(to[j], T.H3L[:, 4 * u:4 * u + 4], T.MS3[:, 4 * j:4 * j + 4]) for j in range(K) if to[j] != core], S.a_h3)
-
-    V.wait_ge(S.a_h3, 2 * len([r for r in served if teams[r][_ks(r, me)] != core]))
-    wait(V, ps3)
-    p = phase()
-    on(p, V.tensor_copy(T.OF3[:], T.H3L[:]))
-    pc = [phase(), phase()]
-    for b, q in enumerate([V, g.scalar]):
-        wait(q, p)
-        q.wait_ge(S.a_tabq, len(onchip))
-        q.wait_ge(S.a_tabo, sum(len(fwd[i]) for i in range(K) if i != k))
-        o, i = T.RES[:, 128 * b:128 * b + 128], T.TAB[:].indirect(T.OF3[:, 8 * b:8 * b + 8])
-        on(pc[b], V.tensor_copy(o, i) if b == 0 else g.scalar.activation(o, i, AF.Copy))
-    wait(g, pc[0], pc[1])
-    each([(T.cores[r], T.LAND[:, 64 * me:64 * me + 64], T.RES[:, 64 * (r % K):64 * (r % K) + 64]) for r in served], S.a_h4)
+    each([(to[j], T.H3L[:, 4 * u:4 * u + 4], T.MS3[:, 4 * j:4 * j + 4]) for j in range(K)], S.a_h3)
     g.wait_ge(S.loc, loc[0])

from concourse.bass import DstId, RemoteDMATransfer
from concourse.mybir import AluOpType as A, AxisListType, ActivationFunctionType as AF

N, K = 16, 4
NCORES = 256
I32, F32, B16, U16 = "int32", "float32", "bfloat16", "uint16"
_SB = {
    "IX": (4, I32), "MP": (1024, I32), "TAB": (8192, B16), "LV": (64, F32), "VV": (2, F32),
    "LM": (8, I32), "H3L": (16, U16), "MS3": (16, U16), "RES": (512, B16), "LAND": (1024, B16), "COL": (256, B16),
    "ONB": (128, B16), "TRI": (128, B16), "IO1": (64, B16), "IOK": (128, B16), "IDF": (128, F32), "SHB": (256, B16),
    "DA": (128, I32), "SE1": (128, B16), "SE2": (128, B16), "SE3": (128, B16), "SEF": (128, F32),
    "PI": (1, I32), "PJ": (2, I32), "MKH": (8, F32), "ONF": (128, F32), "BIG": (128, F32),
    "RAW": (16, I32), "RI": (80, I32), "FA": (16, F32), "PB": (48, B16), "KC": (4, B16),
    "W1": (8, I32), "W2": (8, I32), "W3": (8, I32), "F1": (8, F32), "F2": (8, F32), "F3": (8, F32), "OHA": (112, B16),
    "OHB": (240, B16), "ZA": (128, F32), "ZB": (64, F32), "ZC": (32, F32), "ZD": (16, F32), "RA": (4, F32), "RB": (8, F32),
    "OW": (64, B16), "LF": (512, F32), "LB": (1024, B16), "EF": (32, F32), "EB": (32, B16),
    "OF1": (32, U16), "GG": (256, F32), "MM": (256, F32), "PP": (512, F32),
}
SCRATCH = {n: ("sbuf", [128, w], d) for n, (w, d) in _SB.items()}
SCRATCH.update({"P%d" % i: ("psum", [128, 512], F32) for i in range(6)})
SCRATCH["IXD"] = ("dram", [128, 4], I32)
SCRATCH["IXL"] = ("dram", [K, 128, 4], I32)
PIECES = [(1, 0, 2048, 0), (2, 2048, 2048, 1), (3, 4096, 2048, 2), (1, 6144, 1024, 3), (2, 7168, 1024, 3)]
SEMAPHORES = (["a_mpq", "a_mpo", "a_tabo", "a_h1", "a_h2", "a_rel", "a_h3", "a_h4", "loc", "go",
               "l_ixd", "l_idx", "l_mp", "l_y", "l_in"] + ["a_p%d" % i for i in range(len(PIECES))]
              + ["l_t%d" % i for i in range(4)] + ["c%d" % i for i in range(90)])
_CACHE = {}


def _teams(T, topo):
    if "t" not in _CACHE:
        helpers, servers = [], []
        for c in T.cores:
            chip = [d for d in range(NCORES) if d != c and topo.host(d) == topo.host(c) and topo.chip(d) == topo.chip(c)]
            near = [d for d in chip if topo.die(d) == topo.die(c)]
            far = [d for d in chip if topo.die(d) != topo.die(c)]
            helpers.append([near[0], far[0], near[1], far[1]])
            servers.append([c, near[2], far[2], far[3]])
        _CACHE["t"] = (helpers, servers)
    return _CACHE["t"]


def _kk(r, m):
    return (r // K + m) % K


def _ks(r, m):
    return (m // K + r) % K


def _kt(r, m):
    return (r // K - m // K + 1 + m % 3) % K


def _bits(mask):
    return [i for i in range(16) if (mask >> i) & 1]


def _mask(bits):
    return sum(1 << b for b in bits)


def rank_program(g, core, T, topo):
    teams, servers = _teams(T, topo)
    rank = T.rank_of(core)
    S, V, TE = T.sem, g.vector, g.tensor
    used, loc = [0], [0]

    def phase():
        used[0] += 1
        return {"s": T.sem["c%d" % (used[0] - 1)], "n": 0}

    def on(ph, inst):
        inst.then_inc(ph["s"], 1)
        ph["n"] += 1

    def wait(q, *phs):
        for ph in phs:
            if ph["n"]:
                q.wait_ge(ph["s"], ph["n"])

    def dst(c):
        rid, pid = topo.addr(c, core)
        return DstId(rid=rid, pnc=pid)

    def common(cores):
        m = topo.mask(core, cores[0])
        for d in cores:
            m &= topo.mask(core, d)
        return _bits(m)

    def each(items, sem):
        b = common([d for d, _o, _i in items])
        g.remote_dma_fused([RemoteDMATransfer(dst_ids=[dst(d)], dma_engine_mask=_mask(b[2 * n:2 * n + 2]), remote_sem=sem, src=i, dst=o)
                            for n, (d, o, i) in enumerate(items)], local_sem=S.loc)
        loc[0] += 2 * len(items)

    def same(dests, out, in_, sem, bits):
        g.remote_dma_fused([RemoteDMATransfer(dst_ids=[dst(d) for d in dests], dma_engine_mask=_mask(bits), remote_sem=sem,
                                              srcs=[in_], dsts=[out for _d in dests])], local_sem=S.loc)
        loc[0] += len(bits)

    def tab(i):
        return T.TAB[:, PIECES[i][1]:PIECES[i][1] + PIECES[i][2]]

    def shares(onchip):
        out = []
        for _s, _c, _w, load in PIECES:
            same_load = [i for i in range(len(PIECES)) if PIECES[i][3] == load]
            n, j = len(onchip) // len(same_load), len([1 for i in same_load if i < len(out)])
            out.append(onchip[n * j:n * j + n])
        return out

    def count(C, J, OH, PS, pre):
        z, w = (C - 1) * J, C * J
        pm = phase()
        wait(TE, *pre)
        for d in range(C):
            on(pm, TE.matmul(PS[:, 0:w], T.TRI[:] if d == 0 else T.ONB[:], OH[:, z - d * J:z - d * J + w], d == 0, d == C - 1))
        return pm

    def own(C, J, OH, PS, pm):
        z, w = (C - 1) * J, C * J
        p = phase()
        wait(V, pm)
        on(p, V.tensor_tensor(T.ZA[:, 0:w], PS[:, 0:w], OH[:, z:z + w], A.mult))
        return p

    def ranks(C, J, OH, PS, out, pm):
        p = own(C, J, OH, PS, pm)
        cur, j, n, tmp = T.ZA, J, C * J, [T.ZB, T.ZC, T.ZD]
        while j > 1:
            wait(V, p)
            p = phase()
            o = out if j == 2 else tmp.pop(0)
            on(p, V.tensor_tensor(o[:, 0:n // 2], cur[:, 0:n:2], cur[:, 1:n:2], A.add))
            cur, j, n = o, j // 2, n // 2
        return p

    if rank is not None:
        team = teams[rank]
        par = (rank % K) & 1
        onchip = _bits(topo.mask(core, team[0]))
        nq = len(onchip) // K
        g.sync.dma_start(T.IXD[:], T.idx[:]).then_inc(S.l_ixd, 16)
        g.scalar.dma_start(T.MP[:], T.mp[:]).then_inc(S.l_mp, 16)
        g.sync.dma_start(T.IX[:], T.idx[:]).then_inc(S.l_idx, 16)
        g.scalar.dma_start(T.TAB[:, 0:1024], T.tab[:, 0:1024]).then_inc(S.l_t0, 16)
        g.sync.wait_ge(S.go, 1)
        g.sync.dma_start(T.TAB[:, 1024:2048], T.tab[:, 1024:2048]).then_inc(S.l_t0, 16)
        for i in range(1, 4):
            g.sync.dma_start(T.TAB[:, 2048 * i:2048 * i + 2048], T.tab[:, 2048 * i:2048 * i + 2048]).then_inc(T.sem["l_t%d" % i], 16)
        tload = [32, 16, 16, 16]
        c0, c1 = phase(), phase()
        on(c0, V.memset(T.ONB[:], 1.0))
        on(c0, V.memset(T.ONF[:], 1.0))
        on(c0, V.memset(T.OHA[:, 0:48], 0.0))
        on(c0, V.memset(T.OHB[:, 0:112], 0.0))
        g.wait_ge(S.l_ixd, 16)
        where = [teams[m][_kk(rank, m)] for m in range(N)]
        same(where, T.IXL[rank % K], T.IXD[:], S.a_h1, common(where)[:K])
        g.wait_ge(S.l_mp, 16)
        g.remote_dma_fused([RemoteDMATransfer(dst_ids=[dst(h)], dma_engine_mask=_mask(onchip[nq * i:nq * i + nq]), remote_sem=S.a_mpq,
                                              src=T.MP[:, 256 * i:256 * i + 256], dst=T.MP[:, 256 * i:256 * i + 256])
                            for i, h in enumerate(team)], local_sem=S.loc)
        loc[0] += len(onchip)
        g.sem_inc(S.go, 1)
        on(c1, g.iota(T.IOK[:], [[1, 128]], 0, 0, allow_small_or_imprecise_dtypes=True))
        on(c1, g.iota(T.PI[:], [[0, 1]], 0, 1))
        on(c1, g.iota(T.BIG[:], [[0, 8], [1, 16]], 0, 0, allow_small_or_imprecise_dtypes=True))
        wait(g, c0)
        on(c1, g.affine_select(T.TRI[:], T.ONB[:], [[1, 128]], A.is_ge, 0.0, 0, -1))
        on(c1, g.affine_select(T.IDF[:], T.ONF[:], [[-1, 128]], A.is_equal, 0.0, 0, 1))
        sh = shares(onchip)
        for load in range(4):
            g.wait_ge(T.sem["l_t%d" % load], tload[load])
            ps = [i for i in range(len(PIECES)) if PIECES[i][3] == load]
            g.remote_dma_fused([RemoteDMATransfer(dst_ids=[dst(servers[rank][PIECES[i][0]])], dma_engine_mask=_mask(sh[i]),
                                                  remote_sem=T.sem["a_p%d" % i], src=tab(i), dst=tab(i)) for i in ps],
                               local_sem=S.loc)
            loc[0] += sum(len(sh[i]) for i in ps)
        c2 = phase()
        wait(V, c0, c1)
        on(c2, V.tensor_scalar(T.PJ[:, 0:1], T.PI[:], 3, None, A.arith_shift_right))
        on(c2, V.tensor_scalar(T.PJ[:, 1:2], T.PI[:], 7, None, A.bitwise_and))
        wait(V, c2)
        c3 = phase()
        on(c3, V.tensor_copy(T.VV[:, 0:1], T.PJ[:, 0:1]))
        for h in range(8):
            on(c3, V.tensor_scalar(T.MKH[:, h:h + 1], T.PJ[:, 1:2], float(h), None, A.is_equal))
        wait(V, c3)
        c4 = phase()
        on(c4, V.tensor_scalar(T.SEF[:], T.BIG[:], T.VV[:, 0:1], None, A.is_equal))
        V.wait_ge(S.l_idx, 16)
        p = phase()
        on(p, V.tensor_scalar(T.W1[:, 0:4], T.IX[:], 17, None, A.arith_shift_right))
        wait(V, p)
        p, p2 = phase(), phase()
        for j in range(N):
            on(p, V.tensor_scalar(T.OHA[:, 48 + j:112:16], T.W1[:, 0:4], float(j), None, A.is_equal))
        on(p2, V.tensor_scalar(T.W2[:, 0:4], T.W1[:, 0:4], 1, None, A.bitwise_and))
        on(p2, V.tensor_scalar(T.W3[:, 0:4], T.W1[:, 0:4], 1, None, A.arith_shift_right))
        pm = count(4, N, T.OHA, T.P0, [c0, c1, p])
        wait(V, p2)
        p3, p4 = phase(), phase()
        on(p4, V.tensor_copy(T.F2[:, 0:4], T.W3[:, 0:4]))
        s, o = (-64.0, 63.0) if par else (64.0, -1.0)
        on(p3, V.tensor_scalar(T.F1[:, 0:4], T.W2[:, 0:4], s, o, A.mult, A.add))
        pr = ranks(4, N, T.OHA, T.P0, T.RA, pm)
        wait(V, pr, p3)
        p = phase()
        on(p, V.tensor_tensor(T.F3[:, 0:4], T.F1[:, 0:4], T.RA[:], A.add))
        wait(V, p, p4)
        p, pq = phase(), phase()
        for c in range(4):
            on(p, V.tensor_scalar(T.LF[:, 128 * c:128 * c + 128], T.IOK[:], T.F3[:, c:c + 1], None, A.is_equal))
            on(pq, V.tensor_scalar(T.MM[:, 8 * c:8 * c + 8], T.IOK[:, 0:8], T.F2[:, c:c + 1], None, A.is_equal))
        wait(TE, p)
        pt = phase()
        for c in range(4):
            on(pt, TE.transpose(T.P1[:, 128 * c:128 * c + 128], T.LF[:, 128 * c:128 * c + 128], T.IDF[:]))
        wait(V, pt)
        pt2 = phase()
        on(pt2, V.tensor_copy(T.PP[:], T.P1[:]))
        served = [r for r in range(N) if _kt(r, rank) == 0]
        for i in range(4):
            g.scalar.wait_ge(T.sem["l_t%d" % i], tload[i])
        g.scalar.wait_ge(S.a_h3, 2 * len(served))
        pc = phase()
        on(pc, g.scalar.activation(T.COL[:], T.TAB[:].indirect(T.H3L[:]), AF.Copy))
        wait(g, pc)
        each([(T.cores[r], T.LAND[:, 64 * rank:64 * rank + 64], T.COL[:, 64 * (r % K):64 * (r % K) + 64]) for r in served], S.a_h4)
        V.wait_ge(S.a_rel, len(onchip))
        wait(V, pq)
        p = phase()
        on(p, V.tensor_scalar(T.W1[:], T.LM[:], 13, None, A.arith_shift_right))
        wait(V, p)
        p, p2 = phase(), phase()
        for j in range(N):
            on(p, V.tensor_scalar(T.OHB[:, 112 + j:240:16], T.W1[:], float(16 + j), None, A.is_equal))
        on(p2, V.tensor_scalar(T.F1[:], T.W1[:], 64.0, -1025.0, A.mult, A.add))
        pm = count(8, N, T.OHB, T.P2, [p])
        pr = ranks(8, N, T.OHB, T.P2, T.RB, pm)
        wait(V, pr, p2)
        p = phase()
        on(p, V.tensor_tensor(T.F2[:], T.F1[:], T.RB[:], A.add))
        wait(TE, p, pt2)
        pm = phase()
        for c in range(4):
            on(pm, TE.matmul(T.P3[:, 8 * c:8 * c + 8], T.PP[:, 128 * c:128 * c + 128], T.F2[:], True, True))
        wait(V, pm)
        p = phase()
        on(p, V.tensor_tensor(T.ZB[:, 0:32], T.P3[:, 0:32], T.MM[:, 0:32], A.mult))
        for o, i, n in ((T.ZC, T.ZB, 32), (T.ZD, T.ZC, 16), (T.F1, T.ZD, 8)):
            wait(V, p)
            p = phase()
            on(p, V.tensor_tensor(o[:, 0:n // 2], i[:, 0:n:2], i[:, 1:n:2], A.add))
        wait(V, p)
        p = phase()
        for h in range(8):
            on(p, V.tensor_scalar(T.EF[:, 4 * h:4 * h + 4], T.F1[:, 0:4], T.MKH[:, h:h + 1], None, A.mult))
        wait(TE, c4, p)
        pm = phase()
        on(pm, TE.matmul(T.P4[:, 0:32], T.SEF[:], T.EF[:], True, True))
        wait(V, pm)
        po = phase()
        on(po, V.tensor_copy(T.OF1[:], T.P4[:, 0:32]))
        p1, p2 = phase(), phase()
        for q in (V, g.scalar):
            wait(q, po)
            q.wait_ge(S.a_h4, 2 * N)
        on(p1, V.tensor_copy(T.RES[:, 0:256], T.LAND[:].indirect(T.OF1[:, 0:16])))
        on(p2, g.scalar.activation(T.RES[:, 256:512], T.LAND[:].indirect(T.OF1[:, 16:32]), AF.Copy))
        wait(g.sync, p1)
        g.sync.dma_start(T.y[:, 0:256], T.RES[:, 0:256]).then_inc(S.l_y, 16)
        wait(g.scalar, p2)
        g.scalar.dma_start(T.y[:, 256:512], T.RES[:, 256:512]).then_inc(S.l_y, 16)
        g.sync.wait_ge(S.l_y, 32)
        g.wait_ge(S.loc, loc[0])
        return

    own_server = [r for r in range(N) if core in servers[r]]
    if own_server:
        me = own_server[0]
        mates = servers[me]
        s = mates.index(core)
        served = [r for r in range(N) if _kt(r, me) == s]
        onchip = _bits(topo.mask(core, T.cores[me]))
        sh = shares(onchip)
        others = [d for d in mates if d != core and d != T.cores[me]]
        mine = [i for i in range(len(PIECES)) if PIECES[i][0] == s]
        for i in mine:
            g.wait_ge(T.sem["a_p%d" % i], len(sh[i]))
            same(others, tab(i), tab(i), S.a_tabo, onchip)
        pc = [phase(), phase()]
        for b, q in enumerate([V, g.scalar]):
            for i in mine:
                q.wait_ge(T.sem["a_p%d" % i], len(sh[i]))
            q.wait_ge(S.a_tabo, len(onchip) * (len(PIECES) - len(mine)))
            q.wait_ge(S.a_h3, 2 * len(served))
            o, i = T.COL[:, 128 * b:128 * b + 128], T.TAB[:].indirect(T.H3L[:, 8 * b:8 * b + 8])
            on(pc[b], V.tensor_copy(o, i) if b == 0 else g.scalar.activation(o, i, AF.Copy))
        wait(g, pc[0], pc[1])
        each([(T.cores[r], T.LAND[:, 64 * me:64 * me + 64], T.COL[:, 64 * (r % K):64 * (r % K) + 64]) for r in served], S.a_h4)
        g.wait_ge(S.loc, loc[0])
        return

    mine = [r for r in range(N) if core in teams[r]]
    if not mine:
        return
    me = mine[0]
    team = teams[me]
    k = team.index(core)
    others = [h for h in team if h != core]
    u = me % K
    par = u & 1
    served = [r for r in range(N) if _kk(r, me) == k]
    classes = [m for m in range(N) if _ks(me, m) == k]
    to = [servers[m][_kt(me, m)] for m in classes]
    onchip = _bits(topo.mask(core, T.cores[me]))
    nq = len(onchip) // K

    c0 = phase()
    on(c0, V.memset(T.ONB[:], 1.0))
    on(c0, V.memset(T.SHB[:], 1.0))
    on(c0, V.memset(T.OHA[:, 0:12], 0.0))
    on(c0, V.memset(T.OHB[:, 0:28], 0.0))
    on(c0, V.memset(T.ONF[:], 1.0))
    on(c0, V.memset(T.BIG[0:1, :], 131072.0))
    c1, c1b, c1c = phase(), phase(), phase()
    on(c1, g.iota(T.DA[:], [[-1, 128]], 128, 1))
    on(c1, g.iota(T.PI[:], [[0, 1]], 0, 1))
    on(c1, g.iota(T.IO1[:], [[1, 64]], 1, 0, allow_small_or_imprecise_dtypes=True))
    wait(g, c0)
    on(c1b, g.affine_select(T.TRI[:], T.ONB[:], [[1, 128]], A.is_ge, 0.0, 0, -1))
    on(c1c, g.affine_select(T.IDF[:], T.ONF[:], [[-1, 128]], A.is_equal, 0.0, 0, 1))
    on(c1c, g.iota(T.IOK[:], [[1, 128]], 128, 0, allow_small_or_imprecise_dtypes=True))
    on(c1c, g.affine_select(T.SHB[:], T.SHB[:], [[-64, 2], [1, 128]], A.is_equal, 0.0, 0, -1))
    wait(V, c0, c1)
    c2 = phase()
    on(c2, V.tensor_scalar(T.DA[:], T.DA[:], 15, None, A.bitwise_and))
    on(c2, V.tensor_scalar(T.PJ[:, 0:1], T.PI[:], 4, None, A.arith_shift_right))
    wait(V, c2)
    c3 = phase()
    on(c3, V.tensor_scalar(T.SE1[:], T.DA[:], 0.0, None, A.is_equal))
    on(c3, V.tensor_scalar(T.SE2[:], T.DA[:], 0.0, 128.0, A.is_equal, A.mult))
    on(c3, V.tensor_scalar(T.SE3[:], T.DA[:], 0.0, 32.0, A.is_equal, A.mult))
    for h in range(4):
        on(c3, V.tensor_scalar(T.MKH[:, h:h + 1], T.PJ[:, 0:1], float(h), None, A.is_equal))
    wait(V, c3)
    PG = [T.P4, T.P5]
    wait(TE, c0)
    cg = phase()
    for b in range(2):
        on(cg, TE.matmul(PG[b][:, 0:128], T.ONF[0:1, :], T.BIG[0:1, :], True, False))

    def wrap(PSP, sels, PSW, pre):
        wait(V, pre)
        pe = phase()
        for h in range(4):
            on(pe, V.tensor_scalar(T.EB[0:64, h:32:4], PSP[0:64, 0:8], T.MKH[0:64, h:h + 1], None, A.mult))
        wait(TE, c3, pe)
        pm = phase()
        for i in range(2):
            on(pm, TE.matmul(PSW[:, 0:16], sels[i][0:64, :], T.EB[0:64, 16 * i:16 * i + 16], i == 0, i == 1))
        return pm

    for i in range(K):
        q = g.sync if i < 2 else g.scalar
        if i % 2 == 0:
            q.wait_ge(S.a_h1, K * K)
        blk = 4 * (i ^ (me & 1))
        q.dma_start(T.RAW[:, blk:blk + 4], T.IXL[i]).then_inc(S.l_in, 16)
    V.wait_ge(S.l_in, 16 * K)
    R = [T.RI[:, 16 * i:16 * i + 16] for i in range(5)]
    p, p2 = phase(), phase()
    on(p, V.tensor_scalar(R[0], T.RAW[:], 17, None, A.arith_shift_right))
    on(p2, V.tensor_scalar(R[1], T.RAW[:], 9, 31, A.arith_shift_right, A.bitwise_and))
    wait(V, p)
    p = phase()
    for j in range(K):
        on(p, V.tensor_scalar(T.OHA[:, 12 + j:28:4], T.RI[:, 4 * j:4 * j + 4], float(me), None, A.is_equal))
    on(p2, V.tensor_scalar(R[2], T.RAW[:], 4, 31, A.arith_shift_right, A.bitwise_and))
    on(p2, V.tensor_scalar(R[3], T.RAW[:], 15, None, A.bitwise_and))
    on(p2, V.tensor_scalar(R[4], T.RAW[:], 14, 7, A.arith_shift_right, A.bitwise_and))
    pm = count(4, K, T.OHA, T.P0, [c1b, p])
    wait(V, p2)
    pk, p2 = phase(), phase()
    on(p2, V.tensor_scalar(T.FA[:], R[3], 8.0, 128.0, A.mult, A.add))
    on(pk, V.tensor_copy(T.PB[:, 0:48:3], R[1]))
    on(pk, V.tensor_copy(T.PB[:, 1:48:3], R[2]))
    wait(V, p2)
    on(pk, V.tensor_tensor(T.PB[:, 2:48:3], T.FA[:], R[4], A.add))
    wait(V, p)
    pr = own(4, K, T.OHA, T.P0, pm)
    wait(V, pr)
    pl = [phase() for _ in range(K)]
    for n in range(16):
        j, c = n // 4, n % 4
        on(pl[j], V.tensor_scalar(T.LB[:, 64 * n:64 * n + 64], T.IO1[:], T.ZA[:, 4 * c + j:4 * c + j + 1], None, A.is_equal))
    wait(TE, pk)
    pm = phase()
    for n in range(16):
        j, c = n // 4, n % 4
        if c == 0:
            wait(TE, pl[j])
        on(pm, TE.matmul(T.P1[0:64, j:12:4], T.LB[:, 64 * n:64 * n + 64], T.PB[:, 3 * n:3 * n + 3], c == 0, c == 3))
    pw = wrap(T.P1, [T.SE3, T.SE1], T.P2, pm)
    pb = phase()
    on(pb, V.tensor_copy(T.KC[0:64, :], T.P1[0:64, 8:12]))
    wait(V, pw)
    p = phase()
    on(p, V.tensor_copy(T.OF1[:, 0:16], T.P2[:, 0:16]))
    g.wait_ge(S.a_mpq, nq)
    same(others, T.MP[:, 256 * k:256 * k + 256], T.MP[:, 256 * k:256 * k + 256], S.a_mpo, onchip)

    V.wait_ge(S.a_mpq, nq)
    V.wait_ge(S.a_mpo, (K - 1) * len(onchip))
    wait(V, p)
    pg = [phase(), phase()]
    for b in range(2):
        on(pg[b], V.tensor_copy(T.GG[:, 128 * b:128 * b + 128], T.MP[:].indirect(T.OF1[:, 8 * b:8 * b + 8])))
    wait(TE, c1c, pb)
    pk = phase()
    for n in range(2):
        on(pk, TE.matmul(T.P3[:, 0:2], T.SHB[0:64, 128 * n:128 * n + 128], T.KC[0:64, n:4:2], n == 0, n == 1))
    pgt = [phase(), phase()]
    wait(TE, cg)
    for b in range(2):
        wait(TE, pg[b])
        on(pgt[b], TE.matmul(PG[b][:, 0:128], T.GG[:, 128 * b:128 * b + 128], T.IDF[:], False, True))
    wait(V, c1c, pk)
    pmk = phase()
    for b in range(2):
        on(pmk, V.tensor_scalar(T.MM[:, 128 * b:128 * b + 128], T.IOK[:], T.P3[:, b:b + 1], None, A.is_equal))
    wait(V, pmk)
    pv = phase()
    for b in range(2):
        wait(V, pgt[b])
        p = phase()
        on(p, V.tensor_tensor(T.PP[:, 128 * b:128 * b + 128], PG[b][:, 0:128], T.MM[:, 128 * b:128 * b + 128], A.mult))
        wait(V, p)
        on(pv, V.tensor_reduce(T.VV[:, b:b + 1], T.PP[:, 128 * b:128 * b + 128], AxisListType.X, A.add))
    blk = {r: ((r % K) ^ (me & 1)) // 2 for r in served}
    lv = T.LV[:, 4 * me:4 * me + 1]
    ps2 = phase()
    for r in served:
        if teams[r][0] == core:
            wait(V, pv)
            on(ps2, V.tensor_copy(lv, T.VV[:, blk[r]:blk[r] + 1]))
    wait(g, pv)
    each([(teams[r][0], lv, T.VV[:, blk[r]:blk[r] + 1]) for r in served if teams[r][0] != core], S.a_h2)

    if k == 0:
        n2 = len([m for m in range(N) if teams[m][_kk(me, m)] != core])
        V.wait_ge(S.a_h2, 2 * n2)
        wait(V, ps2)
        p = phase()
        on(p, V.tensor_copy(T.LM[0:64, :], T.LV[0:64, 4 * par:64:8]))
        on(p, V.tensor_copy(T.LM[64:128, :], T.LV[64:128, 4 * (1 - par):64:8]))
        wait(g, p)
        same(others + [T.cores[me]], T.LM[:], T.LM[:], S.a_rel, onchip)
        wait(V, p)
    else:
        V.wait_ge(S.a_rel, len(onchip))

    p, p2 = phase(), phase()
    on(p, V.tensor_scalar(T.W1[:], T.LM[:], 13, None, A.arith_shift_right))
    on(p2, V.tensor_scalar(T.W2[:], T.LM[:], 7, 63, A.arith_shift_right, A.bitwise_and))
    wait(V, p)
    p = phase()
    for j in range(K):
        on(p, V.tensor_scalar(T.OHB[:, 28 + j:60:4], T.W1[:], float(16 + classes[j]), None, A.is_equal))
    on(p2, V.tensor_scalar(T.W3[:], T.LM[:], 127, None, A.bitwise_and))
    pm = count(8, K, T.OHB, T.P0, [p])
    wait(V, p, p2)
    p2 = phase()
    for j in range(K):
        on(p2, V.tensor_tensor(T.OW[:, j:64:8], T.OHB[:, 28 + j:60:4], T.W2[:], A.mult))
        on(p2, V.tensor_tensor(T.OW[:, 4 + j:64:8], T.OHB[:, 28 + j:60:4], T.W3[:], A.mult))
    pr = ranks(8, K, T.OHB, T.P0, T.RB, pm)
    wait(V, pr)
    pl = [phase() for _ in range(4)]
    for c in range(8):
        on(pl[c // 2], V.tensor_scalar(T.LB[:, 64 * c:64 * c + 64], T.IO1[:], T.RB[:, c:c + 1], None, A.is_equal))
    wait(TE, p2)
    pm = phase()
    for c in range(8):
        if c % 2 == 0:
            wait(TE, pl[c // 2])
        on(pm, TE.matmul(T.P1[0:64, 0:8], T.LB[:, 64 * c:64 * c + 64], T.OW[:, 8 * c:8 * c + 8], c == 0, c == 7))
    pw = wrap(T.P1, [T.SE2, T.SE1], T.P2, pm)
    wait(V, pw)
    po = phase()
    on(po, V.tensor_copy(T.MS3[:], T.P2[:, 0:16]))
    wait(g, po)
    each([(to[j], T.H3L[:, 4 * u:4 * u + 4], T.MS3[:, 4 * j:4 * j + 4]) for j in range(K)], S.a_h3)
    g.wait_ge(S.loc, loc[0])
